import numpy as np
import ml_dtypes


def mxq(x, axis, fmt="e4m3"):
    dtype, down = {"e4m3": (ml_dtypes.float8_e4m3fn, 7), "e5m2": (ml_dtypes.float8_e5m2, 14)}[fmt]
    v = np.moveaxis(np.asarray(x, np.float32).astype(ml_dtypes.bfloat16).astype(np.float64), axis, -1)
    blocks = v.reshape(v.shape[:-1] + (-1, 32))
    amax = np.abs(blocks).max(-1, keepdims=True)
    byte = np.maximum(np.where(amax > 0, np.frexp(amax)[1] - 1 + 127, 0) - down, 1)
    scale = np.exp2(byte - 127.0)
    codes = (blocks / scale).astype(np.float32).astype(dtype).astype(np.float64)
    return np.moveaxis((codes * scale).reshape(v.shape), -1, axis)


WIDE = False


def mx_kscale(k):
    if not WIDE:
        return np.ones(k)
    levels = np.array([10, -10, 5, -5, 0])
    if k % 512:
        return np.exp2(np.random.permutation(np.resize(levels, k // 32))).repeat(32)
    a = np.empty((k // 512, 16))
    for p in range(k // 512):
        a[p, :8] = np.random.permutation(np.resize(levels, 8))
        for g in range(8):
            far = levels[np.abs(levels - a[p, g]) >= 10]
            a[p, g + 8] = far[np.random.randint(len(far))]
    return np.exp2(a.ravel()).repeat(32)


def f64(x):
    return np.asarray(x).astype(np.float64)


def striped(idx):
    return np.tile(idx.reshape(-1, 16).T, (8, 1)).astype(np.uint16)


def unstriped(offs):
    return offs[:16].T.reshape(-1).astype(np.int64)


def striped8(idx):
    return np.concatenate([x.reshape(-1, 16).T for x in idx]).astype(np.uint16)


def runs(offs, k):
    lists = np.stack([offs[16 * r : 16 * r + 16].T.reshape(-1) for r in range(8)]).astype(np.int64)
    return lists[np.arange(k) % 512 // 64]


def pack_weight(w):
    k, n = w.shape
    w = f64(np.asarray(w, np.float32).astype(ml_dtypes.bfloat16)).reshape(k // 32, 32, n)
    amax = np.abs(w).max(1)
    byte = np.clip(np.where(amax > 0, np.frexp(amax)[1] - 1 + 127 - 7, 1), 1, 254)
    scaled = (w * np.exp2(127.0 - byte)[:, None, :]).reshape(k, n).astype(np.float32)
    words = np.ascontiguousarray(scaled.reshape(k // 512, 128, 4, n).transpose(0, 1, 3, 2)).astype(ml_dtypes.float8_e4m3fn).view(np.uint8)
    return words, np.ascontiguousarray(byte.astype(np.uint8).reshape(k // 512, 16, n))


def unpack_weight(words, scales):
    g, p, n, _ = words.shape
    vals = np.ascontiguousarray(words).view(ml_dtypes.float8_e4m3fn).astype(np.float64) * np.repeat(np.exp2(scales.astype(np.float64) - 127.0), 8, axis=1)[..., None]
    return vals.transpose(0, 1, 3, 2).reshape(g * 512, n)


def relu(v):
    return np.maximum(v, 0.0)


K, T, S, N, H, U = 1024, 2048, 512, 512, 512, 512


def setup_inputs():
    n = np.random.standard_normal
    s = mx_kscale(K)[:, None]
    u = mx_kscale(H)
    packed_xT = pack_weight(n((K, T)) * s)
    return {
        "x_words": packed_xT[0],
        "x_scales": packed_xT[1],
        "w1": (n((K, H)) / np.sqrt(K) / s).astype(np.float32),
        "mu": (0.5 * n((H, U))).astype(np.float32),
        "rs": (np.random.uniform(0.5, 1.5, (H, U)) * u[:, None]).astype(np.float32),
        "w2": (n((H, N)) / np.sqrt(H) / u[:, None]).astype(np.float32),
        "offs": striped(np.random.permutation(T)[:S]),
        "cl": striped8(np.stack([np.random.permutation(U)[(U * np.random.uniform(0, 1, S) ** 4).astype(np.int64)] for _ in range(8)])),
    }


def reference(x_words, x_scales, w1, mu, rs, w2, offs, cl):
    xq = unpack_weight(x_words, x_scales)[:, unstriped(offs)]
    y = mxq(f64(w1), 0, "e4m3").T @ xq
    z = relu((y - (f64(mu)[np.arange(H)[:, None], runs(cl, H)])) * (f64(rs)[np.arange(H)[:, None], runs(cl, H)]))
    return mxq(f64(w2), 0, "e4m3").T @ mxq(z, 0, "e4m3")

@@ -1,0 +1,193 @@
+from contextlib import ExitStack
+
+import concourse.mybir as mybir
+
+K, T, S, N, H, U = 1024, 2048, 512, 512, 512, 512
+FLOPS = 2 * K * H * S + 2 * H * N * S
+
+F32 = mybir.dt.float32
+BF16 = mybir.dt.bfloat16
+I32 = mybir.dt.int32
+U32 = mybir.dt.uint32
+U16 = mybir.dt.uint16
+U8 = mybir.dt.uint8
+FP8X4 = mybir.dt.float8_e4m3fn_x4
+ALU = mybir.AluOpType
+ACT = mybir.ActivationFunctionType
+
+P = 128
+PACK = 4
+PASSES = K // (P * PACK)
+HALF = S // 2
+LIST_COLS = HALF // 16
+
+
+def tile_picked_clnorm_relu_p_kernel(tc, x_words, x_scales, w1, mu, rs, w2, offs, cl, out):
+    nc = tc.nc
+    with ExitStack() as ctx:
+        sb = ctx.enter_context(tc.tile_pool(name="sb", bufs=1))
+        ps = ctx.enter_context(tc.psum_pool(name="ps", bufs=1))
+
+        def tile(shape, dtype, name):
+            return sb.tile(shape, dtype, name=name, align_bytes=64)
+
+        offs_t = sb.tile([P, S // 16], U16, name="offs_t")
+        cl_t = sb.tile([P, S // 16], U16, name="cl_t")
+        xs_all = tile([P, T], U8, "xs_all")
+        xw_all = [tile([P, T], U32, f"xw_all{g}") for g in range(PASSES)]
+        w1_raw = [tile([P, PACK, H], F32, f"w1_raw{g}") for g in range(PASSES)]
+        w2_raw = [tile([P, PACK, N // 2], F32, f"w2_raw{c}") for c in range(2)]
+        mu_t = [tile([P, U], F32, f"mu{t}") for t in range(PACK)]
+        rs_t = [tile([P, U], F32, f"rs{t}") for t in range(PACK)]
+
+        nc.gpsimd.memset(xs_all[:].bitcast(I32), 0)
+
+        mu_v = mu.rearrange("(p t) u -> p t u", t=PACK)
+        rs_v = rs.rearrange("(p t) u -> p t u", t=PACK)
+        w1_v = w1.rearrange("(g p j) c -> g p j c", g=PASSES, j=PACK)
+        w2_v = w2.rearrange("(p j) c -> p j c", j=PACK)
+
+        nc.sync.dma_start(cl_t[:], cl)
+        for t in range(PACK):
+            nc.sync.dma_start(mu_t[t][:], mu_v[:, t, :])
+        nc.sync.dma_start(w1_raw[0][:], w1_v[0])
+        nc.sync.dma_start(offs_t[:], offs)
+        for t in range(PACK):
+            nc.sync.dma_start(rs_t[t][:], rs_v[:, t, :])
+        for q in range(4):
+            nc.sync.dma_start(
+                xs_all[32 * q : 32 * q + 4 * PASSES, :].bitcast(I32),
+                x_scales[:, 4 * q : 4 * q + 4, :].bitcast(I32),
+            )
+        nc.sync.dma_start(w1_raw[1][:], w1_v[1])
+        for g in range(PASSES):
+            nc.sync.dma_start(xw_all[g][:].bitcast(I32), x_words[g].rearrange("p c r -> p (c r)").bitcast(I32))
+        for c in range(2):
+            nc.sync.dma_start(w2_raw[c][:], w2_v[:, :, c * (N // 2) : (c + 1) * (N // 2)])
+
+        def half_list(lst, h):
+            return lst[:, h * LIST_COLS : (h + 1) * LIST_COLS]
+
+        mu_g = [tile([P, PACK, HALF], F32, f"mu_g{h}") for h in range(2)]
+        rs_g = [tile([P, PACK, HALF], F32, f"rs_g{h}") for h in range(2)]
+        w1_codes = [tile([P, H], U32, f"w1_codes{g}") for g in range(PASSES)]
+        w1_sc = [tile([P, H], U8, f"w1_sc{g}") for g in range(PASSES)]
+        w1_bf = [tile([P, H * PACK], BF16, f"w1_bf{g}") for g in range(PASSES)]
+
+        def look_up(table, dst):
+            for t in range(PACK):
+                for h in range(2):
+                    nc.vector.tensor_copy(dst[h][:, t, :], table[t][:].indirect(half_list(cl_t, h)))
+
+        def cast_w1(g):
+            nc.scalar.activation(
+                out=w1_bf[g][:].rearrange("p (t m j) -> p m j t", t=PACK, j=PACK),
+                in_=w1_raw[g][:].rearrange("p j (m t) -> p m j t", t=PACK),
+                func=ACT.Copy,
+            )
+
+        def quantize(codes, scales, src):
+            nc.vector.quantize_mx(out=codes.bitcast(FP8X4), scales=scales, in_=src)
+
+        def interleave(dst, src, func):
+            nc.scalar.activation(
+                out=dst.rearrange("p (c i t) -> p c t i", i=4, t=PACK),
+                in_=src.rearrange("p t (c i) -> p c t i", i=4),
+                func=func,
+            )
+
+        look_up(mu_t, mu_g)
+        cast_w1(0)
+        look_up(rs_t, rs_g)
+        quantize(w1_codes[0][:], w1_sc[0][:], w1_bf[0][:])
+        xs = tile([P, S], U8, "xs")
+        nc.vector.tensor_copy(xs[:], xs_all[:].indirect(offs_t[:]))
+        cast_w1(1)
+        xw = [[tile([P, HALF], U32, f"xw{g}_{h}") for h in range(2)] for g in range(PASSES)]
+        y = [[ps.tile([P, 512], F32, name=f"y{h}_{t}", tag=f"bank{4 * h + t}") for t in range(PACK)] for h in range(2)]
+
+        def first_product(g, h):
+            nc.vector.tensor_copy(xw[g][h][:], xw_all[g][:].indirect(half_list(offs_t, h)))
+            for t in range(PACK):
+                cols = slice(t * P, (t + 1) * P)
+                nc.tensor.matmul_mx(
+                    out=y[h][t][:, :HALF],
+                    lhsT=w1_codes[g][:, cols].bitcast(FP8X4),
+                    lhsT_scale=w1_sc[g][:, cols],
+                    rhs=xw[g][h][:].bitcast(FP8X4),
+                    rhs_scale=xs[4 * g : P, h * HALF : (h + 1) * HALF],
+                    start=(g == 0),
+                    stop=(g == PASSES - 1),
+                )
+
+        for h in range(2):
+            first_product(0, h)
+        quantize(w1_codes[1][:], w1_sc[1][:], w1_bf[1][:])
+        for h in range(2):
+            first_product(1, h)
+
+        w2_bf = [tile([P, N // 2 * PACK], BF16, f"w2_bf{c}") for c in range(2)]
+        w2_codes = [tile([P, N // 2], U32, f"w2_codes{c}") for c in range(2)]
+        w2_sc = [tile([P, N // 2], U8, f"w2_sc{c}") for c in range(2)]
+        for c in range(2):
+            interleave(w2_bf[c][:], w2_raw[c][:], ACT.Copy)
+
+        centred = [tile([P, PACK, HALF], F32, f"centred{h}") for h in range(2)]
+
+        def centre(h):
+            for t in range(PACK):
+                nc.vector.tensor_tensor(centred[h][:, t, :], y[h][t][:, :HALF], mu_g[h][:, t, :], ALU.subtract)
+
+        out_v = out.rearrange("(a p) s -> p a s", p=P)
+
+        def scale(h, lo, n, name):
+            scaled = tile([P, PACK, n], F32, f"scaled{name}")
+            nc.vector.tensor_tensor(scaled[:], centred[h][:, :, lo : lo + n], rs_g[h][:, :, lo : lo + n], ALU.mult)
+            z_bf = tile([P, n * PACK], BF16, f"z_bf{name}")
+            interleave(z_bf[:], scaled[:], ACT.Relu)
+            return z_bf
+
+        def quantize_z(z_bf, n, name):
+            z_codes = tile([P, n], U32, f"z_codes{name}")
+            z_sc = tile([P, n], U8, f"z_sc{name}")
+            quantize(z_codes[:], z_sc[:], z_bf[:])
+            return z_codes, z_sc
+
+        def second_product(z_mx, s0, n, banks, name):
+            z_codes, z_sc = z_mx
+            for c in range(2):
+                acc = ps.tile([P, 512], F32, name=f"acc{name}_{c}", tag=f"bank{banks[c]}")
+                for b in range(2):
+                    cols = slice(b * P, (b + 1) * P)
+                    nc.tensor.matmul_mx(
+                        out=acc[:, b * n : (b + 1) * n],
+                        lhsT=w2_codes[c][:, cols].bitcast(FP8X4),
+                        lhsT_scale=w2_sc[c][:, cols],
+                        rhs=z_codes[:].bitcast(FP8X4),
+                        rhs_scale=z_sc[:],
+                        start=True,
+                        stop=True,
+                    )
+                res = tile([P, 2, n], F32, f"res{name}_{c}")
+                dst = res[:].rearrange("p a s -> p (a s)")
+                rows = out_v[:, 2 * c : 2 * c + 2, s0 : s0 + n]
+                if c == 1:
+                    nc.scalar.activation(out=dst, in_=acc[:, : 2 * n], func=ACT.Copy)
+                    nc.scalar.dma_start(rows, res[:])
+                else:
+                    nc.vector.tensor_copy(dst, acc[:, : 2 * n])
+                    nc.sync.dma_start(rows, res[:])
+
+        centre(0)
+        z_a = scale(0, 0, HALF, "a")
+        centre(1)
+        for c in range(2):
+            quantize(w2_codes[c][:], w2_sc[c][:], w2_bf[c][:])
+        q_a = quantize_z(z_a, HALF, "a")
+        z_b = scale(1, 0, HALF // 2, "b")
+        z_c = scale(1, HALF // 2, HALF // 2, "c")
+        q_b = quantize_z(z_b, HALF // 2, "b")
+        second_product(q_a, 0, HALF, (0, 1), "a")
+        q_c = quantize_z(z_c, HALF // 2, "c")
+        second_product(q_b, HALF, HALF // 2, (2, 3), "b")
+        second_product(q_c, HALF + HALF // 2, HALF // 2, (4, 5), "c")

@@ -28,8 +28,8 @@ def tile_picked_clnorm_relu_p_kernel(tc, x_words, x_scales, w1, mu, rs, w2, offs
         sb = ctx.enter_context(tc.tile_pool(name="sb", bufs=1))
         ps = ctx.enter_context(tc.psum_pool(name="ps", bufs=1))
 
-        def tile(shape, dtype, name):
-            return sb.tile(shape, dtype, name=name, align_bytes=64)
+        def tile(shape, dtype, name, tag=None):
+            return sb.tile(shape, dtype, name=name, tag=tag or name, align_bytes=64)
 
         offs_t = sb.tile([P, S // 16], U16, name="offs_t")
         cl_t = sb.tile([P, S // 16], U16, name="cl_t")
@@ -47,21 +47,21 @@ def tile_picked_clnorm_relu_p_kernel(tc, x_words, x_scales, w1, mu, rs, w2, offs
         w1_v = w1.rearrange("(g p j) c -> g p j c", g=PASSES, j=PACK)
         w2_v = w2.rearrange("(p j) c -> p j c", j=PACK)
 
-        nc.sync.dma_start(cl_t[:], cl)
-        for t in range(PACK):
-            nc.sync.dma_start(mu_t[t][:], mu_v[:, t, :])
-        nc.sync.dma_start(w1_raw[0][:], w1_v[0])
-        nc.sync.dma_start(offs_t[:], offs)
-        for t in range(PACK):
-            nc.sync.dma_start(rs_t[t][:], rs_v[:, t, :])
         for q in range(4):
-            nc.sync.dma_start(
+            nc.gpsimd.dma_start(
                 xs_all[32 * q : 32 * q + 4 * PASSES, :].bitcast(I32),
                 x_scales[:, 4 * q : 4 * q + 4, :].bitcast(I32),
             )
-        nc.sync.dma_start(w1_raw[1][:], w1_v[1])
+        nc.sync.dma_start(cl_t[:], cl)
+        for t in range(PACK):
+            nc.sync.dma_start(mu_t[t][:], mu_v[:, t, :])
+        nc.sync.dma_start(offs_t[:], offs)
+        for g in range(PASSES):
+            nc.sync.dma_start(w1_raw[g][:], w1_v[g])
         for g in range(PASSES):
             nc.sync.dma_start(xw_all[g][:].bitcast(I32), x_words[g].rearrange("p c r -> p (c r)").bitcast(I32))
+        for t in range(PACK):
+            nc.sync.dma_start(rs_t[t][:], rs_v[:, t, :])
         for c in range(2):
             nc.sync.dma_start(w2_raw[c][:], w2_v[:, :, c * (N // 2) : (c + 1) * (N // 2)])
 
@@ -69,7 +69,6 @@ def tile_picked_clnorm_relu_p_kernel(tc, x_words, x_scales, w1, mu, rs, w2, offs
             return lst[:, h * LIST_COLS : (h + 1) * LIST_COLS]
 
         mu_g = [tile([P, PACK, HALF], F32, f"mu_g{h}") for h in range(2)]
-        rs_g = [tile([P, PACK, HALF], F32, f"rs_g{h}") for h in range(2)]
         w1_codes = [tile([P, H], U32, f"w1_codes{g}") for g in range(PASSES)]
         w1_sc = [tile([P, H], U8, f"w1_sc{g}") for g in range(PASSES)]
         w1_bf = [tile([P, H * PACK], BF16, f"w1_bf{g}") for g in range(PASSES)]
@@ -98,12 +97,11 @@ def tile_picked_clnorm_relu_p_kernel(tc, x_words, x_scales, w1, mu, rs, w2, offs
 
         look_up(mu_t, mu_g)
         cast_w1(0)
-        look_up(rs_t, rs_g)
         quantize(w1_codes[0][:], w1_sc[0][:], w1_bf[0][:])
         xs = tile([P, S], U8, "xs")
         nc.vector.tensor_copy(xs[:], xs_all[:].indirect(offs_t[:]))
         cast_w1(1)
-        xw = [[tile([P, HALF], U32, f"xw{g}_{h}") for h in range(2)] for g in range(PASSES)]
+        xw = [[tile([P, HALF], U32, f"xw{g}_{h}", "xs_all" if g + h == 0 else None) for h in range(2)] for g in range(PASSES)]
         y = [[ps.tile([P, 512], F32, name=f"y{h}_{t}", tag=f"bank{4 * h + t}") for t in range(PACK)] for h in range(2)]
 
         def first_product(g, h):
@@ -140,10 +138,13 @@ def tile_picked_clnorm_relu_p_kernel(tc, x_words, x_scales, w1, mu, rs, w2, offs
 
         out_v = out.rearrange("(a p) s -> p a s", p=P)
 
-        def scale(h, lo, n, name):
-            scaled = tile([P, PACK, n], F32, f"scaled{name}")
-            nc.vector.tensor_tensor(scaled[:], centred[h][:, :, lo : lo + n], rs_g[h][:, :, lo : lo + n], ALU.mult)
-            z_bf = tile([P, n * PACK], BF16, f"z_bf{name}")
+        def scale(h, lo, n, name, scaled_slot, z_slot):
+            scaled = tile([P, PACK, n], F32, f"scaled{name}", scaled_slot)
+            s0 = h * HALF + lo
+            for t in range(PACK):
+                picked = rs_t[t][:].indirect(cl_t[:, s0 // 16 : (s0 + n) // 16])
+                nc.vector.tensor_tensor(scaled[:, t, :], picked, centred[h][:, t, lo : lo + n], ALU.mult)
+            z_bf = tile([P, n * PACK], BF16, f"z_bf{name}", z_slot)
             interleave(z_bf[:], scaled[:], ACT.Relu)
             return z_bf
 
@@ -153,7 +154,7 @@ def tile_picked_clnorm_relu_p_kernel(tc, x_words, x_scales, w1, mu, rs, w2, offs
             quantize(z_codes[:], z_sc[:], z_bf[:])
             return z_codes, z_sc
 
-        def second_product(z_mx, s0, n, banks, name):
+        def second_product(z_mx, s0, n, banks, name, share):
             z_codes, z_sc = z_mx
             for c in range(2):
                 acc = ps.tile([P, 512], F32, name=f"acc{name}_{c}", tag=f"bank{banks[c]}")
@@ -171,7 +172,10 @@ def tile_picked_clnorm_relu_p_kernel(tc, x_words, x_scales, w1, mu, rs, w2, offs
                 res = tile([P, 2, n], F32, f"res{name}_{c}")
                 dst = res[:].rearrange("p a s -> p (a s)")
                 rows = out_v[:, 2 * c : 2 * c + 2, s0 : s0 + n]
-                if c == 1:
+                if not share:
+                    nc.scalar.activation(out=dst, in_=acc[:, : 2 * n], func=ACT.Copy)
+                    nc.sync.dma_start(rows, res[:])
+                elif c == 1:
                     nc.scalar.activation(out=dst, in_=acc[:, : 2 * n], func=ACT.Copy)
                     nc.scalar.dma_start(rows, res[:])
                 else:
@@ -179,15 +183,15 @@ def tile_picked_clnorm_relu_p_kernel(tc, x_words, x_scales, w1, mu, rs, w2, offs
                     nc.sync.dma_start(rows, res[:])
 
         centre(0)
-        z_a = scale(0, 0, HALF, "a")
+        z_a = scale(0, 0, HALF, "a", None, "w2_raw0")
         centre(1)
-        for c in range(2):
-            quantize(w2_codes[c][:], w2_sc[c][:], w2_bf[c][:])
+        quantize(w2_codes[0][:], w2_sc[0][:], w2_bf[0][:])
         q_a = quantize_z(z_a, HALF, "a")
-        z_b = scale(1, 0, HALF // 2, "b")
-        z_c = scale(1, HALF // 2, HALF // 2, "c")
+        z_b = scale(1, 0, HALF // 2, "b", "w2_raw0", "w2_raw1")
+        quantize(w2_codes[1][:], w2_sc[1][:], w2_bf[1][:])
+        z_c = scale(1, HALF // 2, HALF // 2, "c", "w2_bf1", None)
+        second_product(q_a, 0, HALF, (0, 1), "a", False)
         q_b = quantize_z(z_b, HALF // 2, "b")
-        second_product(q_a, 0, HALF, (0, 1), "a")
+        second_product(q_b, HALF, HALF // 2, (2, 3), "b", True)
         q_c = quantize_z(z_c, HALF // 2, "c")
-        second_product(q_b, HALF, HALF // 2, (2, 3), "b")
-        second_product(q_c, HALF + HALF // 2, HALF // 2, (4, 5), "c")
+        second_product(q_c, HALF + HALF // 2, HALF // 2, (4, 5), "c", True)

@@ -19,7 +19,7 @@ P = 128
 PACK = 4
 PASSES = K // (P * PACK)
 HALF = S // 2
-LIST_COLS = HALF // 16
+QUARTER = S // 4
 
 
 def tile_picked_clnorm_relu_p_kernel(tc, x_words, x_scales, w1, mu, rs, w2, offs, cl, out):
@@ -37,8 +37,8 @@ def tile_picked_clnorm_relu_p_kernel(tc, x_words, x_scales, w1, mu, rs, w2, offs
         xw_all = [tile([P, T], U32, f"xw_all{g}") for g in range(PASSES)]
         w1_raw = [tile([P, PACK, H], F32, f"w1_raw{g}") for g in range(PASSES)]
         w2_raw = [tile([P, PACK, N // 2], F32, f"w2_raw{c}") for c in range(2)]
-        mu_t = [tile([P, U], F32, f"mu{t}") for t in range(PACK)]
-        rs_t = [tile([P, U], F32, f"rs{t}") for t in range(PACK)]
+        mu_t = [tile([P, 2 * U], F32, f"mu{t}") for t in range(PACK)]
+        rs_t = [tile([P, 2 * U if t == 0 else U], F32, f"rs{t}") for t in range(PACK)]
 
         nc.gpsimd.memset(xs_all[:].bitcast(I32), 0)
 
@@ -47,36 +47,41 @@ def tile_picked_clnorm_relu_p_kernel(tc, x_words, x_scales, w1, mu, rs, w2, offs
         w1_v = w1.rearrange("(g p j) c -> g p j c", g=PASSES, j=PACK)
         w2_v = w2.rearrange("(p j) c -> p j c", j=PACK)
 
-        for q in range(4):
-            nc.gpsimd.dma_start(
+        def load_scales(queue, q):
+            queue.dma_start(
                 xs_all[32 * q : 32 * q + 4 * PASSES, :].bitcast(I32),
                 x_scales[:, 4 * q : 4 * q + 4, :].bitcast(I32),
             )
+
+        def load_rs(t):
+            nc.sync.dma_start(rs_t[t][:, :U], rs_v[:, t, :])
+
+        def load_w2(c):
+            nc.sync.dma_start(w2_raw[c][:], w2_v[:, :, c * (N // 2) : (c + 1) * (N // 2)])
+
+        for q in range(4):
+            load_scales(nc.gpsimd, q)
         nc.sync.dma_start(cl_t[:], cl)
         for t in range(PACK):
-            nc.sync.dma_start(mu_t[t][:], mu_v[:, t, :])
+            nc.sync.dma_start(mu_t[t][:, :U], mu_v[:, t, :])
+        load_rs(0)
         nc.sync.dma_start(offs_t[:], offs)
         for g in range(PASSES):
             nc.sync.dma_start(w1_raw[g][:], w1_v[g])
         for g in range(PASSES):
             nc.sync.dma_start(xw_all[g][:].bitcast(I32), x_words[g].rearrange("p c r -> p (c r)").bitcast(I32))
-        for t in range(PACK):
-            nc.sync.dma_start(rs_t[t][:], rs_v[:, t, :])
+        for t in range(1, PACK):
+            load_rs(t)
         for c in range(2):
-            nc.sync.dma_start(w2_raw[c][:], w2_v[:, :, c * (N // 2) : (c + 1) * (N // 2)])
+            load_w2(c)
 
-        def half_list(lst, h):
-            return lst[:, h * LIST_COLS : (h + 1) * LIST_COLS]
+        def entries(lst, s0, n):
+            return lst[:, s0 // 16 : (s0 + n) // 16]
 
-        mu_g = [tile([P, PACK, HALF], F32, f"mu_g{h}") for h in range(2)]
+        mu_g = tile([P, PACK, S], F32, "mu_g")
         w1_codes = [tile([P, H], U32, f"w1_codes{g}") for g in range(PASSES)]
         w1_sc = [tile([P, H], U8, f"w1_sc{g}") for g in range(PASSES)]
         w1_bf = [tile([P, H * PACK], BF16, f"w1_bf{g}") for g in range(PASSES)]
-
-        def look_up(table, dst):
-            for t in range(PACK):
-                for h in range(2):
-                    nc.vector.tensor_copy(dst[h][:, t, :], table[t][:].indirect(half_list(cl_t, h)))
 
         def cast_w1(g):
             nc.scalar.activation(
@@ -95,103 +100,109 @@ def tile_picked_clnorm_relu_p_kernel(tc, x_words, x_scales, w1, mu, rs, w2, offs
                 func=func,
             )
 
-        look_up(mu_t, mu_g)
+        for t in range(PACK):
+            nc.vector.tensor_copy(mu_g[:, t, :], mu_t[t][:].indirect(cl_t[:]))
+        rs0_g = tile([P, S], F32, "rs0_g")
+        nc.vector.tensor_copy(rs0_g[:], rs_t[0][:].indirect(cl_t[:]))
         cast_w1(0)
+        cast_w1(1)
         quantize(w1_codes[0][:], w1_sc[0][:], w1_bf[0][:])
         xs = tile([P, S], U8, "xs")
         nc.vector.tensor_copy(xs[:], xs_all[:].indirect(offs_t[:]))
-        cast_w1(1)
-        xw = [[tile([P, HALF], U32, f"xw{g}_{h}", "xs_all" if g + h == 0 else None) for h in range(2)] for g in range(PASSES)]
-        y = [[ps.tile([P, 512], F32, name=f"y{h}_{t}", tag=f"bank{4 * h + t}") for t in range(PACK)] for h in range(2)]
+        y = [[ps.tile([P, 2, HALF], F32, name=f"y{h}_{u}") for u in range(2)] for h in range(2)]
 
         def first_product(g, h):
-            nc.vector.tensor_copy(xw[g][h][:], xw_all[g][:].indirect(half_list(offs_t, h)))
+            words = tile([P, HALF], U32, f"xw{g}_{h}", "xs_all" if g + h == 0 else None)
+            nc.vector.tensor_copy(words[:], xw_all[g][:].indirect(entries(offs_t, h * HALF, HALF)))
             for t in range(PACK):
                 cols = slice(t * P, (t + 1) * P)
                 nc.tensor.matmul_mx(
-                    out=y[h][t][:, :HALF],
+                    out=y[h][t // 2][:, t % 2, :],
                     lhsT=w1_codes[g][:, cols].bitcast(FP8X4),
                     lhsT_scale=w1_sc[g][:, cols],
-                    rhs=xw[g][h][:].bitcast(FP8X4),
+                    rhs=words[:].bitcast(FP8X4),
                     rhs_scale=xs[4 * g : P, h * HALF : (h + 1) * HALF],
-                    start=(g == 0),
-                    stop=(g == PASSES - 1),
+                    start=(g == 0 and t % 2 == 0),
+                    stop=(g == PASSES - 1 and t % 2 == 1),
                 )
 
-        for h in range(2):
-            first_product(0, h)
+        first_product(0, 0)
         quantize(w1_codes[1][:], w1_sc[1][:], w1_bf[1][:])
-        for h in range(2):
-            first_product(1, h)
+        first_product(0, 1)
+        first_product(1, 0)
+        first_product(1, 1)
 
         w2_bf = [tile([P, N // 2 * PACK], BF16, f"w2_bf{c}") for c in range(2)]
         w2_codes = [tile([P, N // 2], U32, f"w2_codes{c}") for c in range(2)]
         w2_sc = [tile([P, N // 2], U8, f"w2_sc{c}") for c in range(2)]
-        for c in range(2):
-            interleave(w2_bf[c][:], w2_raw[c][:], ACT.Copy)
-
-        centred = [tile([P, PACK, HALF], F32, f"centred{h}") for h in range(2)]
-
-        def centre(h):
-            for t in range(PACK):
-                nc.vector.tensor_tensor(centred[h][:, t, :], y[h][t][:, :HALF], mu_g[h][:, t, :], ALU.subtract)
-
         out_v = out.rearrange("(a p) s -> p a s", p=P)
 
-        def scale(h, lo, n, name, scaled_slot, z_slot):
-            scaled = tile([P, PACK, n], F32, f"scaled{name}", scaled_slot)
-            s0 = h * HALF + lo
-            for t in range(PACK):
-                picked = rs_t[t][:].indirect(cl_t[:, s0 // 16 : (s0 + n) // 16])
-                nc.vector.tensor_tensor(scaled[:, t, :], picked, centred[h][:, t, lo : lo + n], ALU.mult)
-            z_bf = tile([P, n * PACK], BF16, f"z_bf{name}", z_slot)
-            interleave(z_bf[:], scaled[:], ACT.Relu)
+        def centre(centred, h):
+            for u in range(2):
+                planes = slice(2 * u, 2 * u + 2)
+                nc.vector.tensor_tensor(centred[:, planes, :], y[h][u][:], mu_g[:, planes, h * HALF : (h + 1) * HALF], ALU.subtract)
+
+        def scale(scaled, centred, s0, n):
+            nc.vector.tensor_tensor(scaled[:, 0, :], rs0_g[:, s0 : s0 + n], centred[:, 0, :], ALU.mult)
+            for t in range(1, PACK):
+                nc.vector.tensor_tensor(scaled[:, t, :], rs_t[t][:].indirect(entries(cl_t, s0, n)), centred[:, t, :], ALU.mult)
+
+        def relu(scaled, n, name, slot=None):
+            z_bf = tile([P, n * PACK], BF16, name, slot)
+            interleave(z_bf[:], scaled, ACT.Relu)
             return z_bf
 
-        def quantize_z(z_bf, n, name):
-            z_codes = tile([P, n], U32, f"z_codes{name}")
-            z_sc = tile([P, n], U8, f"z_sc{name}")
+        def quantize_z(z_bf, s0, n):
+            z_codes = tile([P, n], U32, f"z_codes{s0}")
+            z_sc = tile([P, n], U8, f"z_sc{s0}")
             quantize(z_codes[:], z_sc[:], z_bf[:])
-            return z_codes, z_sc
+            return z_codes, z_sc, s0, n
 
-        def second_product(z_mx, s0, n, banks, name, share):
-            z_codes, z_sc = z_mx
-            for c in range(2):
-                acc = ps.tile([P, 512], F32, name=f"acc{name}_{c}", tag=f"bank{banks[c]}")
-                for b in range(2):
-                    cols = slice(b * P, (b + 1) * P)
-                    nc.tensor.matmul_mx(
-                        out=acc[:, b * n : (b + 1) * n],
-                        lhsT=w2_codes[c][:, cols].bitcast(FP8X4),
-                        lhsT_scale=w2_sc[c][:, cols],
-                        rhs=z_codes[:].bitcast(FP8X4),
-                        rhs_scale=z_sc[:],
-                        start=True,
-                        stop=True,
-                    )
-                res = tile([P, 2, n], F32, f"res{name}_{c}")
-                dst = res[:].rearrange("p a s -> p (a s)")
-                rows = out_v[:, 2 * c : 2 * c + 2, s0 : s0 + n]
-                if not share:
-                    nc.scalar.activation(out=dst, in_=acc[:, : 2 * n], func=ACT.Copy)
-                    nc.sync.dma_start(rows, res[:])
-                elif c == 1:
-                    nc.scalar.activation(out=dst, in_=acc[:, : 2 * n], func=ACT.Copy)
-                    nc.scalar.dma_start(rows, res[:])
-                else:
-                    nc.vector.tensor_copy(dst, acc[:, : 2 * n])
-                    nc.sync.dma_start(rows, res[:])
+        def second_product(z_mx, c, bank):
+            z_codes, z_sc, s0, n = z_mx
+            acc = ps.tile([P, 512], F32, name=f"acc{s0}_{c}", tag=bank)
+            for b in range(2):
+                cols = slice(b * P, (b + 1) * P)
+                nc.tensor.matmul_mx(
+                    out=acc[:, b * n : (b + 1) * n],
+                    lhsT=w2_codes[c][:, cols].bitcast(FP8X4),
+                    lhsT_scale=w2_sc[c][:, cols],
+                    rhs=z_codes[:].bitcast(FP8X4),
+                    rhs_scale=z_sc[:],
+                    start=True,
+                    stop=True,
+                )
+            return acc, s0, n, c
 
-        centre(0)
-        z_a = scale(0, 0, HALF, "a", None, "w2_raw0")
-        centre(1)
+        def store(product, copy_out, queue, slot=None):
+            acc, s0, n, c = product
+            res = tile([P, 2, n], F32, f"res{s0}_{c}", slot)
+            copy_out(res[:].rearrange("p a s -> p (a s)"), acc[:, : 2 * n])
+            queue.dma_start(out_v[:, 2 * c : 2 * c + 2, s0 : s0 + n], res[:])
+
+        for c in range(2):
+            interleave(w2_bf[c][:], w2_raw[c][:], ACT.Copy)
+        c_a = tile([P, PACK, HALF], F32, "centred0")
+        centre(c_a, 0)
+        s_a = tile([P, PACK, HALF], F32, "scaled0")
+        scale(s_a, c_a, 0, HALF)
+        z_a = relu(s_a[:], HALF, "z_a", "w2_raw0")
+        c_b = tile([P, PACK, HALF], F32, "centred1")
+        centre(c_b, 1)
         quantize(w2_codes[0][:], w2_sc[0][:], w2_bf[0][:])
-        q_a = quantize_z(z_a, HALF, "a")
-        z_b = scale(1, 0, HALF // 2, "b", "w2_raw0", "w2_raw1")
+        q_a = quantize_z(z_a, 0, HALF)
+        s_b = tile([P, PACK, QUARTER], F32, "scaled1", "scaled0")
+        scale(s_b, c_b[:, :, :QUARTER], HALF, QUARTER)
+        z_b = relu(s_b[:], QUARTER, "z_b", "w2_raw1")
         quantize(w2_codes[1][:], w2_sc[1][:], w2_bf[1][:])
-        z_c = scale(1, HALF // 2, HALF // 2, "c", "w2_bf1", None)
-        second_product(q_a, 0, HALF, (0, 1), "a", False)
-        q_b = quantize_z(z_b, HALF // 2, "b")
-        second_product(q_b, HALF, HALF // 2, (2, 3), "b", True)
-        q_c = quantize_z(z_c, HALF // 2, "c")
-        second_product(q_c, HALF + HALF // 2, HALF // 2, (4, 5), "c", True)
+        s_c = tile([P, PACK, QUARTER], F32, "scaled2", "w2_bf1")
+        scale(s_c, c_b[:, :, QUARTER:], HALF + QUARTER, QUARTER)
+        z_c = relu(s_c[:], QUARTER, "z_c")
+        store(second_product(q_a, 0, "acc0"), nc.scalar.copy, nc.sync)
+        store(second_product(q_a, 1, "acc1"), nc.scalar.copy, nc.sync)
+        q_b = quantize_z(z_b, HALF, QUARTER)
+        store(second_product(q_b, 0, "acc2"), nc.vector.tensor_copy, nc.sync)
+        store(second_product(q_b, 1, "acc3"), nc.scalar.copy, nc.scalar)
+        q_c = quantize_z(z_c, HALF + QUARTER, QUARTER)
+        store(second_product(q_c, 0, "y0_0"), nc.vector.tensor_copy, nc.sync)
+        store(second_product(q_c, 1, "y0_1"), nc.scalar.copy, nc.scalar)

@@ -200,6 +200,17 @@ def tile_picked_clnorm_relu_p_kernel(tc, x_words, x_scales, w1, mu, rs, w2, offs
         z_c = relu(s_c[:], QUARTER, "z_c")
         store(second_product(q_a, 0, "acc0"), nc.scalar.copy, nc.sync)
         store(second_product(q_a, 1, "acc1"), nc.scalar.copy, nc.sync)
+        for u in range(2):
+            idle = ps.tile([P, 512], F32, name=f"warm{u}", tag=f"y1_{u}")
+            nc.tensor.matmul_mx(
+                out=idle[:],
+                lhsT=w2_codes[1][:, :P].bitcast(FP8X4),
+                lhsT_scale=w2_sc[1][:, :P],
+                rhs=w1_codes[1][:].bitcast(FP8X4),
+                rhs_scale=w1_sc[1][:],
+                start=True,
+                stop=True,
+            )
         q_b = quantize_z(z_b, HALF, QUARTER)
         store(second_product(q_b, 0, "acc2"), nc.vector.tensor_copy, nc.sync)
         store(second_product(q_b, 1, "acc3"), nc.scalar.copy, nc.scalar)

@@ -1,6 +1,7 @@
 from contextlib import ExitStack
 
 import concourse.mybir as mybir
+from concourse.masks import make_identity
 
 K, T, S, N, H, U = 1024, 2048, 512, 512, 512, 512
 FLOPS = 2 * K * H * S + 2 * H * N * S
@@ -38,124 +39,138 @@ def tile_picked_clnorm_relu_p_kernel(tc, x_words, x_scales, w1, mu, rs, w2, offs
         w1_raw = [tile([P, PACK, H], F32, f"w1_raw{g}") for g in range(PASSES)]
         w2_raw = [tile([P, PACK, N // 2], F32, f"w2_raw{c}") for c in range(2)]
         mu_t = [tile([P, 2 * U], F32, f"mu{t}") for t in range(PACK)]
-        rs_t = [tile([P, 2 * U if t == 0 else U], F32, f"rs{t}") for t in range(PACK)]
+        rs_t = [tile([P, 2 * U], F32, f"rs{t}") for t in range(PACK)]
+        ident = tile([P, P], F32, "ident")
 
-        nc.gpsimd.memset(xs_all[:].bitcast(I32), 0)
+        one = tile([P, 1], F32, "one")
+        minus_one = tile([P, 1], F32, "minus_one")
+        nc.vector.memset(one[:], 1.0)
+        nc.scalar.activation(minus_one[:], one[:], ACT.Copy, scale=-1.0)
+        nc.vector.memset(xs_all[:].bitcast(I32), 0)
+        make_identity(nc, ident[:])
 
         mu_v = mu.rearrange("(p t) u -> p t u", t=PACK)
         rs_v = rs.rearrange("(p t) u -> p t u", t=PACK)
         w1_v = w1.rearrange("(g p j) c -> g p j c", g=PASSES, j=PACK)
         w2_v = w2.rearrange("(p j) c -> p j c", j=PACK)
 
-        def load_scales(queue, q):
-            queue.dma_start(
+        for q in range(4):
+            nc.gpsimd.dma_start(
                 xs_all[32 * q : 32 * q + 4 * PASSES, :].bitcast(I32),
                 x_scales[:, 4 * q : 4 * q + 4, :].bitcast(I32),
             )
-
-        def load_rs(t):
-            nc.sync.dma_start(rs_t[t][:, :U], rs_v[:, t, :])
-
-        def load_w2(c):
-            nc.sync.dma_start(w2_raw[c][:], w2_v[:, :, c * (N // 2) : (c + 1) * (N // 2)])
-
-        for q in range(4):
-            load_scales(nc.gpsimd, q)
         nc.sync.dma_start(cl_t[:], cl)
         for t in range(PACK):
+            nc.sync.dma_start(rs_t[t][:, :U], rs_v[:, t, :])
+        for t in range(PACK):
             nc.sync.dma_start(mu_t[t][:, :U], mu_v[:, t, :])
-        load_rs(0)
+        nc.sync.dma_start(w1_raw[0][:], w1_v[0])
         nc.sync.dma_start(offs_t[:], offs)
-        for g in range(PASSES):
-            nc.sync.dma_start(w1_raw[g][:], w1_v[g])
+        nc.sync.dma_start(w1_raw[1][:], w1_v[1])
         for g in range(PASSES):
             nc.sync.dma_start(xw_all[g][:].bitcast(I32), x_words[g].rearrange("p c r -> p (c r)").bitcast(I32))
-        for t in range(1, PACK):
-            load_rs(t)
         for c in range(2):
-            load_w2(c)
+            nc.sync.dma_start(w2_raw[c][:], w2_v[:, :, c * (N // 2) : (c + 1) * (N // 2)])
 
         def entries(lst, s0, n):
             return lst[:, s0 // 16 : (s0 + n) // 16]
 
-        mu_g = tile([P, PACK, S], F32, "mu_g")
-        w1_codes = [tile([P, H], U32, f"w1_codes{g}") for g in range(PASSES)]
+        def look_up(table, t, name):
+            picked = tile([P, S], F32, name)
+            if t % 2 == 0:
+                nc.scalar.activation(picked[:], table[:].indirect(cl_t[:]), ACT.Copy)
+            else:
+                nc.vector.tensor_copy(picked[:], table[:].indirect(cl_t[:]))
+            return picked
+
+        def turn(picked, name, bank):
+            turned = ps.tile([P, 4, P], F32, name=name, tag=bank)
+            for q in range(4):
+                nc.tensor.transpose(turned[:, q, :], picked[:, q * P : (q + 1) * P], ident[:])
+            return turned
+
+        def add_turned(dst, src, start, stop):
+            nc.tensor.matmul(dst, lhsT=src, rhs=ident[:], start=start, stop=stop, is_transpose=True)
+
+        rs_g = [look_up(rs_t[t], t, f"rs_g{t}") for t in range(PACK)]
+        mu_g = [look_up(mu_t[t], t, f"mu_g{t}") for t in range(PACK)]
+        rs_tok = tile([P, 4, PACK, P], F32, "rs_tok")
+        for t in range(PACK):
+            nc.scalar.copy(rs_tok[:, :, t, :], turn(rs_g[t], f"rs_turned{t}", f"z{t}")[:])
+        z_pre = [ps.tile([P, PACK, P], F32, name=f"z_pre{q}", tag=f"z{q}") for q in range(4)]
+        def mu_term(t, shift):
+            nc.vector.scalar_tensor_tensor(
+                shift, turn(mu_g[t], f"mu_turned{t}", f"y{t}")[:], minus_one[:], rs_tok[:, :, t, :], ALU.mult, ALU.mult
+            )
+            for q in range(4):
+                add_turned(z_pre[q][:, t, :], shift[:, q, :], t == 0, False)
+
+        for t in range(2):
+            mu_term(t, tile([P, 4, P], F32, f"shift{t}")[:])
+
+        w1_codes = []
         w1_sc = [tile([P, H], U8, f"w1_sc{g}") for g in range(PASSES)]
         w1_bf = [tile([P, H * PACK], BF16, f"w1_bf{g}") for g in range(PASSES)]
-
-        def cast_w1(g):
-            nc.scalar.activation(
-                out=w1_bf[g][:].rearrange("p (t m j) -> p m j t", t=PACK, j=PACK),
-                in_=w1_raw[g][:].rearrange("p j (m t) -> p m j t", t=PACK),
-                func=ACT.Copy,
-            )
 
         def quantize(codes, scales, src):
             nc.vector.quantize_mx(out=codes.bitcast(FP8X4), scales=scales, in_=src)
 
-        def interleave(dst, src, func):
-            nc.scalar.activation(
-                out=dst.rearrange("p (c i t) -> p c t i", i=4, t=PACK),
-                in_=src.rearrange("p t (c i) -> p c t i", i=4),
-                func=func,
-            )
+        def interleaved(dst, src):
+            return dst.rearrange("p (c i t) -> p c t i", i=4, t=PACK), src.rearrange("p t (c i) -> p c t i", i=4)
 
-        for t in range(PACK):
-            nc.vector.tensor_copy(mu_g[:, t, :], mu_t[t][:].indirect(cl_t[:]))
-        rs0_g = tile([P, S], F32, "rs0_g")
-        nc.vector.tensor_copy(rs0_g[:], rs_t[0][:].indirect(cl_t[:]))
-        cast_w1(0)
-        cast_w1(1)
-        quantize(w1_codes[0][:], w1_sc[0][:], w1_bf[0][:])
+        nc.vector.tensor_copy(*interleaved(w1_bf[0][:], w1_raw[0][:]))
+        nc.scalar.activation(*interleaved(w1_bf[1][:], w1_raw[1][:]), ACT.Copy)
         xs = tile([P, S], U8, "xs")
         nc.vector.tensor_copy(xs[:], xs_all[:].indirect(offs_t[:]))
-        y = [[ps.tile([P, 2, HALF], F32, name=f"y{h}_{u}") for u in range(2)] for h in range(2)]
+        w1_codes.append(tile([P, H], U32, "w1_codes0"))
+        quantize(w1_codes[0][:], w1_sc[0][:], w1_bf[0][:])
+        late_shift = tile([P, 2, 4, P], F32, "late_shift", "w1_raw0")
+        for t in range(2, PACK):
+            mu_term(t, late_shift[:, t - 2, :, :])
+        y = [ps.tile([P, H], F32, name=f"y{q}", tag=f"y{q}") for q in range(4)]
 
         def first_product(g, h):
-            words = tile([P, HALF], U32, f"xw{g}_{h}", "xs_all" if g + h == 0 else None)
+            words = tile([P, HALF], U32, f"xw{g}_{h}")
             nc.vector.tensor_copy(words[:], xw_all[g][:].indirect(entries(offs_t, h * HALF, HALF)))
-            for t in range(PACK):
-                cols = slice(t * P, (t + 1) * P)
+            for b in range(2):
+                q = 2 * h + b
                 nc.tensor.matmul_mx(
-                    out=y[h][t // 2][:, t % 2, :],
-                    lhsT=w1_codes[g][:, cols].bitcast(FP8X4),
-                    lhsT_scale=w1_sc[g][:, cols],
-                    rhs=words[:].bitcast(FP8X4),
-                    rhs_scale=xs[4 * g : P, h * HALF : (h + 1) * HALF],
-                    start=(g == 0 and t % 2 == 0),
-                    stop=(g == PASSES - 1 and t % 2 == 1),
+                    out=y[q][:],
+                    lhsT=words[:, b * P : (b + 1) * P].bitcast(FP8X4),
+                    lhsT_scale=xs[4 * g : P, q * P : (q + 1) * P],
+                    rhs=w1_codes[g][:].bitcast(FP8X4),
+                    rhs_scale=w1_sc[g][:],
+                    start=(g == 0),
+                    stop=(g == PASSES - 1),
                 )
 
-        first_product(0, 0)
+        for h in range(2):
+            first_product(0, h)
+        w1_codes.append(tile([P, H], U32, "w1_codes1", "xw_all0"))
         quantize(w1_codes[1][:], w1_sc[1][:], w1_bf[1][:])
-        first_product(0, 1)
-        first_product(1, 0)
-        first_product(1, 1)
+        for h in range(2):
+            first_product(1, h)
 
         w2_bf = [tile([P, N // 2 * PACK], BF16, f"w2_bf{c}") for c in range(2)]
         w2_codes = [tile([P, N // 2], U32, f"w2_codes{c}") for c in range(2)]
         w2_sc = [tile([P, N // 2], U8, f"w2_sc{c}") for c in range(2)]
         out_v = out.rearrange("(a p) s -> p a s", p=P)
 
-        def centre(centred, h):
-            for u in range(2):
-                planes = slice(2 * u, 2 * u + 2)
-                nc.vector.tensor_tensor(centred[:, planes, :], y[h][u][:], mu_g[:, planes, h * HALF : (h + 1) * HALF], ALU.subtract)
+        def scale(q):
+            scaled = tile([P, PACK, P], F32, f"scaled{q}")
+            nc.vector.tensor_tensor(scaled[:], y[q][:].rearrange("p (m t) -> p t m", t=PACK), rs_tok[:, q, :, :], ALU.mult)
+            for t in range(PACK):
+                add_turned(z_pre[q][:, t, :], scaled[:, t, :], False, t == PACK - 1)
 
-        def scale(scaled, centred, s0, n):
-            nc.vector.tensor_tensor(scaled[:, 0, :], rs0_g[:, s0 : s0 + n], centred[:, 0, :], ALU.mult)
-            for t in range(1, PACK):
-                nc.vector.tensor_tensor(scaled[:, t, :], rs_t[t][:].indirect(entries(cl_t, s0, n)), centred[:, t, :], ALU.mult)
-
-        def relu(scaled, n, name, slot=None):
-            z_bf = tile([P, n * PACK], BF16, name, slot)
-            interleave(z_bf[:], scaled, ACT.Relu)
-            return z_bf
+        def relu(q, z_bf):
+            nc.scalar.activation(
+                out=z_bf.rearrange("p (s t) -> p s t", t=PACK), in_=z_pre[q][:].rearrange("p t s -> p s t"), func=ACT.Relu
+            )
 
         def quantize_z(z_bf, s0, n):
             z_codes = tile([P, n], U32, f"z_codes{s0}")
             z_sc = tile([P, n], U8, f"z_sc{s0}")
-            quantize(z_codes[:], z_sc[:], z_bf[:])
+            quantize(z_codes[:], z_sc[:], z_bf)
             return z_codes, z_sc, s0, n
 
         def second_product(z_mx, c, bank):
@@ -174,46 +189,29 @@ def tile_picked_clnorm_relu_p_kernel(tc, x_words, x_scales, w1, mu, rs, w2, offs
                 )
             return acc, s0, n, c
 
-        def store(product, copy_out, queue, slot=None):
+        def store(product, copy_out, queue):
             acc, s0, n, c = product
-            res = tile([P, 2, n], F32, f"res{s0}_{c}", slot)
+            res = tile([P, 2, n], F32, f"res{s0}_{c}")
             copy_out(res[:].rearrange("p a s -> p (a s)"), acc[:, : 2 * n])
             queue.dma_start(out_v[:, 2 * c : 2 * c + 2, s0 : s0 + n], res[:])
 
-        for c in range(2):
-            interleave(w2_bf[c][:], w2_raw[c][:], ACT.Copy)
-        c_a = tile([P, PACK, HALF], F32, "centred0")
-        centre(c_a, 0)
-        s_a = tile([P, PACK, HALF], F32, "scaled0")
-        scale(s_a, c_a, 0, HALF)
-        z_a = relu(s_a[:], HALF, "z_a", "w2_raw0")
-        c_b = tile([P, PACK, HALF], F32, "centred1")
-        centre(c_b, 1)
+        nc.scalar.activation(*interleaved(w2_bf[0][:], w2_raw[0][:]), ACT.Copy)
+        z_bf = tile([P, 4, QUARTER * PACK], BF16, "z_bf")
+        scale(0)
+        scale(1)
         quantize(w2_codes[0][:], w2_sc[0][:], w2_bf[0][:])
-        q_a = quantize_z(z_a, 0, HALF)
-        s_b = tile([P, PACK, QUARTER], F32, "scaled1", "scaled0")
-        scale(s_b, c_b[:, :, :QUARTER], HALF, QUARTER)
-        z_b = relu(s_b[:], QUARTER, "z_b", "w2_raw1")
+        scale(2)
+        scale(3)
+        for q in range(4):
+            relu(q, z_bf[:, q, :])
+        q_a = quantize_z(z_bf[:, :2, :].rearrange("p q c -> p (q c)"), 0, HALF)
+        nc.vector.tensor_copy(*interleaved(w2_bf[1][:], w2_raw[1][:]))
+        q_b = quantize_z(z_bf[:, 2, :], HALF, QUARTER)
         quantize(w2_codes[1][:], w2_sc[1][:], w2_bf[1][:])
-        s_c = tile([P, PACK, QUARTER], F32, "scaled2", "w2_bf1")
-        scale(s_c, c_b[:, :, QUARTER:], HALF + QUARTER, QUARTER)
-        z_c = relu(s_c[:], QUARTER, "z_c")
-        store(second_product(q_a, 0, "acc0"), nc.scalar.copy, nc.sync)
-        store(second_product(q_a, 1, "acc1"), nc.scalar.copy, nc.sync)
-        for u in range(2):
-            idle = ps.tile([P, 512], F32, name=f"warm{u}", tag=f"y1_{u}")
-            nc.tensor.matmul_mx(
-                out=idle[:],
-                lhsT=w2_codes[1][:, :P].bitcast(FP8X4),
-                lhsT_scale=w2_sc[1][:, :P],
-                rhs=w1_codes[1][:].bitcast(FP8X4),
-                rhs_scale=w1_sc[1][:],
-                start=True,
-                stop=True,
-            )
-        q_b = quantize_z(z_b, HALF, QUARTER)
-        store(second_product(q_b, 0, "acc2"), nc.vector.tensor_copy, nc.sync)
-        store(second_product(q_b, 1, "acc3"), nc.scalar.copy, nc.scalar)
-        q_c = quantize_z(z_c, HALF + QUARTER, QUARTER)
-        store(second_product(q_c, 0, "y0_0"), nc.vector.tensor_copy, nc.sync)
-        store(second_product(q_c, 1, "y0_1"), nc.scalar.copy, nc.scalar)
+        q_c = quantize_z(z_bf[:, 3, :], HALF + QUARTER, QUARTER)
+        store(second_product(q_a, 0, "y0"), nc.scalar.copy, nc.sync)
+        store(second_product(q_b, 0, "y2"), nc.scalar.copy, nc.sync)
+        store(second_product(q_a, 1, "y1"), nc.scalar.copy, nc.sync)
+        store(second_product(q_b, 1, "y3"), nc.vector.tensor_copy, nc.sync)
+        store(second_product(q_c, 0, "z0"), nc.vector.tensor_copy, nc.sync)
+        store(second_product(q_c, 1, "z1"), nc.scalar.copy, nc.scalar)

@@ -55,17 +55,17 @@ def tile_picked_clnorm_relu_p_kernel(tc, x_words, x_scales, w1, mu, rs, w2, offs
         w2_v = w2.rearrange("(p j) c -> p j c", j=PACK)
 
         for q in range(4):
-            nc.gpsimd.dma_start(
+            (nc.gpsimd if q < 2 else nc.scalar).dma_start(
                 xs_all[32 * q : 32 * q + 4 * PASSES, :].bitcast(I32),
                 x_scales[:, 4 * q : 4 * q + 4, :].bitcast(I32),
             )
         nc.sync.dma_start(cl_t[:], cl)
         for t in range(PACK):
             nc.sync.dma_start(rs_t[t][:, :U], rs_v[:, t, :])
+        nc.sync.dma_start(offs_t[:], offs)
         for t in range(PACK):
             nc.sync.dma_start(mu_t[t][:, :U], mu_v[:, t, :])
         nc.sync.dma_start(w1_raw[0][:], w1_v[0])
-        nc.sync.dma_start(offs_t[:], offs)
         nc.sync.dma_start(w1_raw[1][:], w1_v[1])
         for g in range(PASSES):
             nc.sync.dma_start(xw_all[g][:].bitcast(I32), x_words[g].rearrange("p c r -> p (c r)").bitcast(I32))
@@ -105,12 +105,15 @@ def tile_picked_clnorm_relu_p_kernel(tc, x_words, x_scales, w1, mu, rs, w2, offs
             for q in range(4):
                 add_turned(z_pre[q][:, t, :], shift[:, q, :], t == 0, False)
 
-        for t in range(2):
-            mu_term(t, tile([P, 4, P], F32, f"shift{t}")[:])
+        xs = tile([P, S], U8, "xs", "mu3")
+        nc.vector.tensor_copy(xs[:], xs_all[:].indirect(offs_t[:]))
+        shift = tile([P, PACK, 4, P], F32, "shift", "xs_all")
+        for t in range(PACK):
+            mu_term(t, shift[:, t, :, :])
 
         w1_codes = []
         w1_sc = [tile([P, H], U8, f"w1_sc{g}") for g in range(PASSES)]
-        w1_bf = [tile([P, H * PACK], BF16, f"w1_bf{g}") for g in range(PASSES)]
+        w1_bf = [tile([P, H * PACK], BF16, f"w1_bf{g}", ("mu_g2", "mu2")[g]) for g in range(PASSES)]
 
         def quantize(codes, scales, src):
             nc.vector.quantize_mx(out=codes.bitcast(FP8X4), scales=scales, in_=src)
@@ -118,20 +121,14 @@ def tile_picked_clnorm_relu_p_kernel(tc, x_words, x_scales, w1, mu, rs, w2, offs
         def interleaved(dst, src):
             return dst.rearrange("p (c i t) -> p c t i", i=4, t=PACK), src.rearrange("p t (c i) -> p c t i", i=4)
 
-        nc.vector.tensor_copy(*interleaved(w1_bf[0][:], w1_raw[0][:]))
-        nc.scalar.activation(*interleaved(w1_bf[1][:], w1_raw[1][:]), ACT.Copy)
-        xs = tile([P, S], U8, "xs")
-        nc.vector.tensor_copy(xs[:], xs_all[:].indirect(offs_t[:]))
+        for g in range(PASSES):
+            nc.scalar.activation(*interleaved(w1_bf[g][:], w1_raw[g][:]), ACT.Copy)
         w1_codes.append(tile([P, H], U32, "w1_codes0"))
         quantize(w1_codes[0][:], w1_sc[0][:], w1_bf[0][:])
-        late_shift = tile([P, 2, 4, P], F32, "late_shift", "w1_raw0")
-        for t in range(2, PACK):
-            mu_term(t, late_shift[:, t - 2, :, :])
         y = [ps.tile([P, H], F32, name=f"y{q}", tag=f"y{q}") for q in range(4)]
 
-        def first_product(g, h):
-            words = tile([P, HALF], U32, f"xw{g}_{h}")
-            nc.vector.tensor_copy(words[:], xw_all[g][:].indirect(entries(offs_t, h * HALF, HALF)))
+        def first_product(g, h, words):
+            nc.vector.tensor_copy(words, xw_all[g][:].indirect(entries(offs_t, h * HALF, HALF)))
             for b in range(2):
                 q = 2 * h + b
                 nc.tensor.matmul_mx(
@@ -144,15 +141,17 @@ def tile_picked_clnorm_relu_p_kernel(tc, x_words, x_scales, w1, mu, rs, w2, offs
                     stop=(g == PASSES - 1),
                 )
 
+        xw0 = tile([P, S], U32, "xw0", "mu_g2")
         for h in range(2):
-            first_product(0, h)
+            first_product(0, h, xw0[:, h * HALF : (h + 1) * HALF])
         w1_codes.append(tile([P, H], U32, "w1_codes1", "xw_all0"))
         quantize(w1_codes[1][:], w1_sc[1][:], w1_bf[1][:])
+        xw1 = tile([P, S], U32, "xw1", "mu2")
         for h in range(2):
-            first_product(1, h)
+            first_product(1, h, xw1[:, h * HALF : (h + 1) * HALF])
 
-        w2_bf = [tile([P, N // 2 * PACK], BF16, f"w2_bf{c}") for c in range(2)]
-        w2_codes = [tile([P, N // 2], U32, f"w2_codes{c}") for c in range(2)]
+        w2_bf = []
+        w2_codes = []
         w2_sc = [tile([P, N // 2], U8, f"w2_sc{c}") for c in range(2)]
         out_v = out.rearrange("(a p) s -> p a s", p=P)
 
@@ -195,18 +194,22 @@ def tile_picked_clnorm_relu_p_kernel(tc, x_words, x_scales, w1, mu, rs, w2, offs
             copy_out(res[:].rearrange("p a s -> p (a s)"), acc[:, : 2 * n])
             queue.dma_start(out_v[:, 2 * c : 2 * c + 2, s0 : s0 + n], res[:])
 
+        w2_bf.append(tile([P, N // 2 * PACK], BF16, "w2_bf0", "w1_raw1"))
         nc.scalar.activation(*interleaved(w2_bf[0][:], w2_raw[0][:]), ACT.Copy)
         z_bf = tile([P, 4, QUARTER * PACK], BF16, "z_bf")
         scale(0)
         scale(1)
+        w2_codes.append(tile([P, N // 2], U32, "w2_codes0", "scaled0"))
         quantize(w2_codes[0][:], w2_sc[0][:], w2_bf[0][:])
         scale(2)
         scale(3)
         for q in range(4):
             relu(q, z_bf[:, q, :])
         q_a = quantize_z(z_bf[:, :2, :].rearrange("p q c -> p (q c)"), 0, HALF)
+        w2_bf.append(tile([P, N // 2 * PACK], BF16, "w2_bf1", "scaled2"))
         nc.vector.tensor_copy(*interleaved(w2_bf[1][:], w2_raw[1][:]))
         q_b = quantize_z(z_bf[:, 2, :], HALF, QUARTER)
+        w2_codes.append(tile([P, N // 2], U32, "w2_codes1"))
         quantize(w2_codes[1][:], w2_sc[1][:], w2_bf[1][:])
         q_c = quantize_z(z_bf[:, 3, :], HALF + QUARTER, QUARTER)
         store(second_product(q_a, 0, "y0"), nc.scalar.copy, nc.sync)

@@ -21,6 +21,7 @@ PACK = 4
 PASSES = K // (P * PACK)
 HALF = S // 2
 QUARTER = S // 4
+CAST_SPLIT = 3 * H // 4
 
 
 def tile_picked_clnorm_relu_p_kernel(tc, x_words, x_scales, w1, mu, rs, w2, offs, cl, out):
@@ -55,16 +56,17 @@ def tile_picked_clnorm_relu_p_kernel(tc, x_words, x_scales, w1, mu, rs, w2, offs
         w2_v = w2.rearrange("(p j) c -> p j c", j=PACK)
 
         for q in range(4):
-            (nc.gpsimd if q < 2 else nc.scalar).dma_start(
+            (nc.gpsimd if q < 3 else nc.scalar).dma_start(
                 xs_all[32 * q : 32 * q + 4 * PASSES, :].bitcast(I32),
                 x_scales[:, 4 * q : 4 * q + 4, :].bitcast(I32),
             )
+        nc.sync.dma_start(mu_t[0][:, :U], mu_v[:, 0, :])
         nc.sync.dma_start(cl_t[:], cl)
-        for t in range(PACK):
-            nc.sync.dma_start(rs_t[t][:, :U], rs_v[:, t, :])
+        for t in range(1, PACK):
+            nc.sync.dma_start(mu_t[t][:, :U], mu_v[:, t, :])
         nc.sync.dma_start(offs_t[:], offs)
         for t in range(PACK):
-            nc.sync.dma_start(mu_t[t][:, :U], mu_v[:, t, :])
+            nc.sync.dma_start(rs_t[t][:, :U], rs_v[:, t, :])
         nc.sync.dma_start(w1_raw[0][:], w1_v[0])
         nc.sync.dma_start(w1_raw[1][:], w1_v[1])
         for g in range(PASSES):
@@ -92,28 +94,26 @@ def tile_picked_clnorm_relu_p_kernel(tc, x_words, x_scales, w1, mu, rs, w2, offs
         def add_turned(dst, src, start, stop):
             nc.tensor.matmul(dst, lhsT=src, rhs=ident[:], start=start, stop=stop, is_transpose=True)
 
-        rs_g = [look_up(rs_t[t], t, f"rs_g{t}") for t in range(PACK)]
         mu_g = [look_up(mu_t[t], t, f"mu_g{t}") for t in range(PACK)]
+        rs_g = [look_up(rs_t[t], t, f"rs_g{t}") for t in range(PACK)]
+        mu_turned = [turn(mu_g[t], f"mu_turned{t}", f"y{t}") for t in range(PACK)]
         rs_tok = tile([P, 4, PACK, P], F32, "rs_tok")
         for t in range(PACK):
             nc.scalar.copy(rs_tok[:, :, t, :], turn(rs_g[t], f"rs_turned{t}", f"z{t}")[:])
         z_pre = [ps.tile([P, PACK, P], F32, name=f"z_pre{q}", tag=f"z{q}") for q in range(4)]
         def mu_term(t, shift):
             nc.vector.scalar_tensor_tensor(
-                shift, turn(mu_g[t], f"mu_turned{t}", f"y{t}")[:], minus_one[:], rs_tok[:, :, t, :], ALU.mult, ALU.mult
+                shift, mu_turned[t][:], minus_one[:], rs_tok[:, :, t, :], ALU.mult, ALU.mult
             )
             for q in range(4):
                 add_turned(z_pre[q][:, t, :], shift[:, q, :], t == 0, False)
 
-        xs = tile([P, S], U8, "xs", "mu3")
-        nc.vector.tensor_copy(xs[:], xs_all[:].indirect(offs_t[:]))
-        shift = tile([P, PACK, 4, P], F32, "shift", "xs_all")
         for t in range(PACK):
-            mu_term(t, shift[:, t, :, :])
+            mu_term(t, tile([P, 4, P], F32, f"shift{t}")[:])
 
         w1_codes = []
         w1_sc = [tile([P, H], U8, f"w1_sc{g}") for g in range(PASSES)]
-        w1_bf = [tile([P, H * PACK], BF16, f"w1_bf{g}", ("mu_g2", "mu2")[g]) for g in range(PASSES)]
+        w1_bf = [tile([P, H * PACK], BF16, f"w1_bf{g}", ("rs_g3", "w1_raw0")[g]) for g in range(PASSES)]
 
         def quantize(codes, scales, src):
             nc.vector.quantize_mx(out=codes.bitcast(FP8X4), scales=scales, in_=src)
@@ -121,9 +121,12 @@ def tile_picked_clnorm_relu_p_kernel(tc, x_words, x_scales, w1, mu, rs, w2, offs
         def interleaved(dst, src):
             return dst.rearrange("p (c i t) -> p c t i", i=4, t=PACK), src.rearrange("p t (c i) -> p c t i", i=4)
 
-        for g in range(PASSES):
-            nc.scalar.activation(*interleaved(w1_bf[g][:], w1_raw[g][:]), ACT.Copy)
-        w1_codes.append(tile([P, H], U32, "w1_codes0"))
+        nc.scalar.activation(*interleaved(w1_bf[0][:, : CAST_SPLIT * PACK], w1_raw[0][:, :, :CAST_SPLIT]), ACT.Copy)
+        nc.vector.tensor_copy(*interleaved(w1_bf[0][:, CAST_SPLIT * PACK :], w1_raw[0][:, :, CAST_SPLIT:]))
+        nc.scalar.activation(*interleaved(w1_bf[1][:], w1_raw[1][:]), ACT.Copy)
+        xs = tile([P, S], U8, "xs", "shift0")
+        nc.vector.tensor_copy(xs[:], xs_all[:].indirect(offs_t[:]))
+        w1_codes.append(tile([P, H], U32, "w1_codes0", "xs_all"))
         quantize(w1_codes[0][:], w1_sc[0][:], w1_bf[0][:])
         y = [ps.tile([P, H], F32, name=f"y{q}", tag=f"y{q}") for q in range(4)]
 
@@ -141,12 +144,12 @@ def tile_picked_clnorm_relu_p_kernel(tc, x_words, x_scales, w1, mu, rs, w2, offs
                     stop=(g == PASSES - 1),
                 )
 
-        xw0 = tile([P, S], U32, "xw0", "mu_g2")
+        xw0 = tile([P, S], U32, "xw0", "rs_g3")
         for h in range(2):
             first_product(0, h, xw0[:, h * HALF : (h + 1) * HALF])
         w1_codes.append(tile([P, H], U32, "w1_codes1", "xw_all0"))
         quantize(w1_codes[1][:], w1_sc[1][:], w1_bf[1][:])
-        xw1 = tile([P, S], U32, "xw1", "mu2")
+        xw1 = tile([P, S], U32, "xw1", "w1_raw0")
         for h in range(2):
             first_product(1, h, xw1[:, h * HALF : (h + 1) * HALF])
 

@@ -21,7 +21,6 @@ PACK = 4
 PASSES = K // (P * PACK)
 HALF = S // 2
 QUARTER = S // 4
-CAST_SPLIT = 3 * H // 4
 
 
 def tile_picked_clnorm_relu_p_kernel(tc, x_words, x_scales, w1, mu, rs, w2, offs, cl, out):
@@ -60,13 +59,13 @@ def tile_picked_clnorm_relu_p_kernel(tc, x_words, x_scales, w1, mu, rs, w2, offs
                 xs_all[32 * q : 32 * q + 4 * PASSES, :].bitcast(I32),
                 x_scales[:, 4 * q : 4 * q + 4, :].bitcast(I32),
             )
-        nc.sync.dma_start(mu_t[0][:, :U], mu_v[:, 0, :])
+        nc.sync.dma_start(rs_t[0][:, :U], rs_v[:, 0, :])
         nc.sync.dma_start(cl_t[:], cl)
         for t in range(1, PACK):
-            nc.sync.dma_start(mu_t[t][:, :U], mu_v[:, t, :])
-        nc.sync.dma_start(offs_t[:], offs)
-        for t in range(PACK):
             nc.sync.dma_start(rs_t[t][:, :U], rs_v[:, t, :])
+            nc.sync.dma_start(mu_t[t - 1][:, :U], mu_v[:, t - 1, :])
+        nc.sync.dma_start(mu_t[PACK - 1][:, :U], mu_v[:, PACK - 1, :])
+        nc.sync.dma_start(offs_t[:], offs)
         nc.sync.dma_start(w1_raw[0][:], w1_v[0])
         nc.sync.dma_start(w1_raw[1][:], w1_v[1])
         for g in range(PASSES):
@@ -79,41 +78,41 @@ def tile_picked_clnorm_relu_p_kernel(tc, x_words, x_scales, w1, mu, rs, w2, offs
 
         def look_up(table, t, name):
             picked = tile([P, S], F32, name)
-            if t % 2 == 0:
+            if t != 1:
                 nc.scalar.activation(picked[:], table[:].indirect(cl_t[:]), ACT.Copy)
             else:
                 nc.vector.tensor_copy(picked[:], table[:].indirect(cl_t[:]))
             return picked
 
-        def turn(picked, name, bank):
+        def turn(blocks, name, bank):
             turned = ps.tile([P, 4, P], F32, name=name, tag=bank)
-            for q in range(4):
-                nc.tensor.transpose(turned[:, q, :], picked[:, q * P : (q + 1) * P], ident[:])
+            for i, block in enumerate(blocks):
+                nc.tensor.transpose(turned[:, i, :], block, ident[:])
             return turned
 
         def add_turned(dst, src, start, stop):
             nc.tensor.matmul(dst, lhsT=src, rhs=ident[:], start=start, stop=stop, is_transpose=True)
 
-        mu_g = [look_up(mu_t[t], t, f"mu_g{t}") for t in range(PACK)]
         rs_g = [look_up(rs_t[t], t, f"rs_g{t}") for t in range(PACK)]
-        mu_turned = [turn(mu_g[t], f"mu_turned{t}", f"y{t}") for t in range(PACK)]
-        rs_tok = tile([P, 4, PACK, P], F32, "rs_tok")
+        rs_turned = [turn([rs_g[t][:, q * P : (q + 1) * P] for q in range(4)], f"rs_turned{t}", f"y{t}") for t in range(PACK)]
+        mu_rs = [tile([P, S], F32, f"mu_rs{t}") for t in range(PACK)]
         for t in range(PACK):
-            nc.scalar.copy(rs_tok[:, :, t, :], turn(rs_g[t], f"rs_turned{t}", f"z{t}")[:])
+            nc.vector.tensor_tensor(mu_rs[t][:], mu_t[t][:].indirect(cl_t[:]), rs_g[t][:], ALU.mult)
+        rs_tok = tile([P, 4, PACK, P], F32, "rs_tok", "rs3")
+        for t in range(PACK):
+            nc.scalar.copy(rs_tok[:, :, t, :], rs_turned[t][:])
+        mu_turned = [turn([mu_rs[t][:, q * P : (q + 1) * P] for q in range(4)], f"mu_turned{t}", f"z{t}") for t in range(PACK)]
+        shift = [tile([P, 4, P], F32, f"shift{t}") for t in range(PACK)]
+        for t in range(PACK):
+            nc.scalar.activation(shift[t][:], mu_turned[t][:], ACT.Copy, scale=minus_one[:])
         z_pre = [ps.tile([P, PACK, P], F32, name=f"z_pre{q}", tag=f"z{q}") for q in range(4)]
-        def mu_term(t, shift):
-            nc.vector.scalar_tensor_tensor(
-                shift, mu_turned[t][:], minus_one[:], rs_tok[:, :, t, :], ALU.mult, ALU.mult
-            )
-            for q in range(4):
-                add_turned(z_pre[q][:, t, :], shift[:, q, :], t == 0, False)
-
         for t in range(PACK):
-            mu_term(t, tile([P, 4, P], F32, f"shift{t}")[:])
+            for q in range(4):
+                add_turned(z_pre[q][:, t, :], shift[t][:, q, :], t == 0, False)
 
         w1_codes = []
         w1_sc = [tile([P, H], U8, f"w1_sc{g}") for g in range(PASSES)]
-        w1_bf = [tile([P, H * PACK], BF16, f"w1_bf{g}", ("rs_g3", "w1_raw0")[g]) for g in range(PASSES)]
+        w1_bf = [tile([P, H * PACK], BF16, f"w1_bf{g}", ("mu3", "mu_rs3")[g]) for g in range(PASSES)]
 
         def quantize(codes, scales, src):
             nc.vector.quantize_mx(out=codes.bitcast(FP8X4), scales=scales, in_=src)
@@ -121,10 +120,9 @@ def tile_picked_clnorm_relu_p_kernel(tc, x_words, x_scales, w1, mu, rs, w2, offs
         def interleaved(dst, src):
             return dst.rearrange("p (c i t) -> p c t i", i=4, t=PACK), src.rearrange("p t (c i) -> p c t i", i=4)
 
-        nc.scalar.activation(*interleaved(w1_bf[0][:, : CAST_SPLIT * PACK], w1_raw[0][:, :, :CAST_SPLIT]), ACT.Copy)
-        nc.vector.tensor_copy(*interleaved(w1_bf[0][:, CAST_SPLIT * PACK :], w1_raw[0][:, :, CAST_SPLIT:]))
+        nc.vector.tensor_copy(*interleaved(w1_bf[0][:], w1_raw[0][:]))
         nc.scalar.activation(*interleaved(w1_bf[1][:], w1_raw[1][:]), ACT.Copy)
-        xs = tile([P, S], U8, "xs", "shift0")
+        xs = tile([P, S], U8, "xs", "w1_raw0")
         nc.vector.tensor_copy(xs[:], xs_all[:].indirect(offs_t[:]))
         w1_codes.append(tile([P, H], U32, "w1_codes0", "xs_all"))
         quantize(w1_codes[0][:], w1_sc[0][:], w1_bf[0][:])
@@ -144,12 +142,12 @@ def tile_picked_clnorm_relu_p_kernel(tc, x_words, x_scales, w1, mu, rs, w2, offs
                     stop=(g == PASSES - 1),
                 )
 
-        xw0 = tile([P, S], U32, "xw0", "rs_g3")
+        xw0 = tile([P, S], U32, "xw0", "mu3")
         for h in range(2):
             first_product(0, h, xw0[:, h * HALF : (h + 1) * HALF])
-        w1_codes.append(tile([P, H], U32, "w1_codes1", "xw_all0"))
+        w1_codes.append(tile([P, H], U32, "w1_codes1"))
         quantize(w1_codes[1][:], w1_sc[1][:], w1_bf[1][:])
-        xw1 = tile([P, S], U32, "xw1", "w1_raw0")
+        xw1 = tile([P, S], U32, "xw1")
         for h in range(2):
             first_product(1, h, xw1[:, h * HALF : (h + 1) * HALF])
 

@@ -167,33 +167,32 @@ def tile_picked_clnorm_relu_p_kernel(tc, x_words, x_scales, w1, mu, rs, w2, offs
                 out=z_bf.rearrange("p (s t) -> p s t", t=PACK), in_=z_pre[q][:].rearrange("p t s -> p s t"), func=ACT.Relu
             )
 
-        def quantize_z(z_bf, s0, n):
-            z_codes = tile([P, n], U32, f"z_codes{s0}")
-            z_sc = tile([P, n], U8, f"z_sc{s0}")
-            quantize(z_codes[:], z_sc[:], z_bf)
-            return z_codes, z_sc, s0, n
+        z_codes = tile([P, S], U32, "z_codes")
+        z_sc = tile([P, S], U8, "z_sc")
 
-        def second_product(z_mx, c, bank):
-            z_codes, z_sc, s0, n = z_mx
-            acc = ps.tile([P, 512], F32, name=f"acc{s0}_{c}", tag=bank)
-            for b in range(2):
-                cols = slice(b * P, (b + 1) * P)
+        def quantize_z(z_bf, s0, n):
+            quantize(z_codes[:, s0 : s0 + n], z_sc[:, s0 : s0 + n], z_bf)
+
+        def second_product(s0, n, blocks, bank):
+            acc = ps.tile([P, 512], F32, name=f"acc{s0}_{blocks[0]}", tag=bank)
+            for i, b in enumerate(blocks):
+                cols = slice(b % 2 * P, (b % 2 + 1) * P)
                 nc.tensor.matmul_mx(
-                    out=acc[:, b * n : (b + 1) * n],
-                    lhsT=w2_codes[c][:, cols].bitcast(FP8X4),
-                    lhsT_scale=w2_sc[c][:, cols],
-                    rhs=z_codes[:].bitcast(FP8X4),
-                    rhs_scale=z_sc[:],
+                    out=acc[:, i * n : (i + 1) * n],
+                    lhsT=w2_codes[b // 2][:, cols].bitcast(FP8X4),
+                    lhsT_scale=w2_sc[b // 2][:, cols],
+                    rhs=z_codes[:, s0 : s0 + n].bitcast(FP8X4),
+                    rhs_scale=z_sc[:, s0 : s0 + n],
                     start=True,
                     stop=True,
                 )
-            return acc, s0, n, c
+            return acc, s0, n, blocks
 
         def store(product, copy_out, queue):
-            acc, s0, n, c = product
-            res = tile([P, 2, n], F32, f"res{s0}_{c}")
-            copy_out(res[:].rearrange("p a s -> p (a s)"), acc[:, : 2 * n])
-            queue.dma_start(out_v[:, 2 * c : 2 * c + 2, s0 : s0 + n], res[:])
+            acc, s0, n, blocks = product
+            res = tile([P, len(blocks), n], F32, f"res{s0}_{blocks[0]}")
+            copy_out(res[:].rearrange("p a s -> p (a s)"), acc[:, : len(blocks) * n])
+            queue.dma_start(out_v[:, blocks[0] : blocks[-1] + 1, s0 : s0 + n], res[:])
 
         w2_bf.append(tile([P, N // 2 * PACK], BF16, "w2_bf0", "w1_raw1"))
         nc.scalar.activation(*interleaved(w2_bf[0][:], w2_raw[0][:]), ACT.Copy)
@@ -206,16 +205,15 @@ def tile_picked_clnorm_relu_p_kernel(tc, x_words, x_scales, w1, mu, rs, w2, offs
         scale(3)
         for q in range(4):
             relu(q, z_bf[:, q, :])
-        q_a = quantize_z(z_bf[:, :2, :].rearrange("p q c -> p (q c)"), 0, HALF)
+        quantize_z(z_bf[:, :2, :].rearrange("p q c -> p (q c)"), 0, HALF)
         w2_bf.append(tile([P, N // 2 * PACK], BF16, "w2_bf1", "scaled2"))
         nc.vector.tensor_copy(*interleaved(w2_bf[1][:], w2_raw[1][:]))
-        q_b = quantize_z(z_bf[:, 2, :], HALF, QUARTER)
+        quantize_z(z_bf[:, 2, :], HALF, QUARTER)
         w2_codes.append(tile([P, N // 2], U32, "w2_codes1"))
         quantize(w2_codes[1][:], w2_sc[1][:], w2_bf[1][:])
-        q_c = quantize_z(z_bf[:, 3, :], HALF + QUARTER, QUARTER)
-        store(second_product(q_a, 0, "y0"), nc.scalar.copy, nc.sync)
-        store(second_product(q_b, 0, "y2"), nc.scalar.copy, nc.sync)
-        store(second_product(q_a, 1, "y1"), nc.scalar.copy, nc.sync)
-        store(second_product(q_b, 1, "y3"), nc.vector.tensor_copy, nc.sync)
-        store(second_product(q_c, 0, "z0"), nc.vector.tensor_copy, nc.sync)
-        store(second_product(q_c, 1, "z1"), nc.scalar.copy, nc.scalar)
+        quantize_z(z_bf[:, 3, :], HALF + QUARTER, QUARTER)
+        store(second_product(0, HALF, (0, 1), "y0"), nc.scalar.copy, nc.sync)
+        store(second_product(HALF, QUARTER, (0, 1), "y2"), nc.scalar.copy, nc.sync)
+        store(second_product(HALF + QUARTER, QUARTER, (0, 1), "z0"), nc.scalar.copy, nc.sync)
+        store(second_product(0, S, (2,), "y1"), nc.vector.tensor_copy, nc.sync)
+        store(second_product(0, S, (3,), "y3"), nc.scalar.copy, nc.scalar)

@@ -212,8 +212,10 @@ def tile_picked_clnorm_relu_p_kernel(tc, x_words, x_scales, w1, mu, rs, w2, offs
         w2_codes.append(tile([P, N // 2], U32, "w2_codes1"))
         quantize(w2_codes[1][:], w2_sc[1][:], w2_bf[1][:])
         quantize_z(z_bf[:, 3, :], HALF + QUARTER, QUARTER)
-        store(second_product(0, HALF, (0, 1), "y0"), nc.scalar.copy, nc.sync)
+        store(second_product(0, HALF, (0,), "y0"), nc.scalar.copy, nc.sync)
+        store(second_product(0, HALF, (1,), "y1"), nc.scalar.copy, nc.sync)
         store(second_product(HALF, QUARTER, (0, 1), "y2"), nc.scalar.copy, nc.sync)
+        store(second_product(0, HALF, (2,), "y3"), nc.scalar.copy, nc.sync)
         store(second_product(HALF + QUARTER, QUARTER, (0, 1), "z0"), nc.scalar.copy, nc.sync)
-        store(second_product(0, S, (2,), "y1"), nc.vector.tensor_copy, nc.sync)
-        store(second_product(0, S, (3,), "y3"), nc.scalar.copy, nc.scalar)
+        store(second_product(0, S, (3,), "z1"), nc.vector.tensor_copy, nc.sync)
+        store(second_product(HALF, HALF, (2,), "z2"), nc.scalar.copy, nc.scalar)

@@ -55,7 +55,7 @@ def tile_picked_clnorm_relu_p_kernel(tc, x_words, x_scales, w1, mu, rs, w2, offs
         w2_v = w2.rearrange("(p j) c -> p j c", j=PACK)
 
         for q in range(4):
-            (nc.gpsimd if q < 3 else nc.scalar).dma_start(
+            (nc.scalar if q == 0 else nc.gpsimd).dma_start(
                 xs_all[32 * q : 32 * q + 4 * PASSES, :].bitcast(I32),
                 x_scales[:, 4 * q : 4 * q + 4, :].bitcast(I32),
             )

@@ -21,6 +21,7 @@ PACK = 4
 PASSES = K // (P * PACK)
 HALF = S // 2
 QUARTER = S // 4
+W2_GROUPS = ((0, 1, 2), (3,))
 
 
 def tile_picked_clnorm_relu_p_kernel(tc, x_words, x_scales, w1, mu, rs, w2, offs, cl, out):
@@ -37,7 +38,7 @@ def tile_picked_clnorm_relu_p_kernel(tc, x_words, x_scales, w1, mu, rs, w2, offs
         xs_all = tile([P, T], U8, "xs_all")
         xw_all = [tile([P, T], U32, f"xw_all{g}") for g in range(PASSES)]
         w1_raw = [tile([P, PACK, H], F32, f"w1_raw{g}") for g in range(PASSES)]
-        w2_raw = [tile([P, PACK, N // 2], F32, f"w2_raw{c}") for c in range(2)]
+        w2_raw = [tile([P, PACK, P], F32, f"w2_raw{b}") for b in range(4)]
         mu_t = [tile([P, 2 * U], F32, f"mu{t}") for t in range(PACK)]
         rs_t = [tile([P, 2 * U], F32, f"rs{t}") for t in range(PACK)]
         ident = tile([P, P], F32, "ident")
@@ -70,8 +71,8 @@ def tile_picked_clnorm_relu_p_kernel(tc, x_words, x_scales, w1, mu, rs, w2, offs
         nc.sync.dma_start(w1_raw[1][:], w1_v[1])
         for g in range(PASSES):
             nc.sync.dma_start(xw_all[g][:].bitcast(I32), x_words[g].rearrange("p c r -> p (c r)").bitcast(I32))
-        for c in range(2):
-            nc.sync.dma_start(w2_raw[c][:], w2_v[:, :, c * (N // 2) : (c + 1) * (N // 2)])
+        for b in range(4):
+            nc.sync.dma_start(w2_raw[b][:], w2_v[:, :, b * P : (b + 1) * P])
 
         def entries(lst, s0, n):
             return lst[:, s0 // 16 : (s0 + n) // 16]
@@ -128,10 +129,9 @@ def tile_picked_clnorm_relu_p_kernel(tc, x_words, x_scales, w1, mu, rs, w2, offs
         quantize(w1_codes[0][:], w1_sc[0][:], w1_bf[0][:])
         y = [ps.tile([P, H], F32, name=f"y{q}", tag=f"y{q}") for q in range(4)]
 
-        def first_product(g, h, words):
-            nc.vector.tensor_copy(words, xw_all[g][:].indirect(entries(offs_t, h * HALF, HALF)))
-            for b in range(2):
-                q = 2 * h + b
+        def first_product(g, quarters, words):
+            nc.vector.tensor_copy(words, xw_all[g][:].indirect(entries(offs_t, quarters[0] * P, len(quarters) * P)))
+            for b, q in enumerate(quarters):
                 nc.tensor.matmul_mx(
                     out=y[q][:],
                     lhsT=words[:, b * P : (b + 1) * P].bitcast(FP8X4),
@@ -143,17 +143,17 @@ def tile_picked_clnorm_relu_p_kernel(tc, x_words, x_scales, w1, mu, rs, w2, offs
                 )
 
         xw0 = tile([P, S], U32, "xw0", "mu3")
-        for h in range(2):
-            first_product(0, h, xw0[:, h * HALF : (h + 1) * HALF])
+        first_product(0, (0,), xw0[:, :P])
+        first_product(0, (1,), xw0[:, P:HALF])
+        first_product(0, (2, 3), xw0[:, HALF:])
         w1_codes.append(tile([P, H], U32, "w1_codes1"))
         quantize(w1_codes[1][:], w1_sc[1][:], w1_bf[1][:])
-        xw1 = tile([P, S], U32, "xw1")
-        for h in range(2):
-            first_product(1, h, xw1[:, h * HALF : (h + 1) * HALF])
+        first_product(1, (0,), tile([P, P], U32, "xw1_0")[:])
+        first_product(1, (1, 2, 3), tile([P, 3 * P], U32, "xw1_1")[:])
 
         w2_bf = []
         w2_codes = []
-        w2_sc = [tile([P, N // 2], U8, f"w2_sc{c}") for c in range(2)]
+        w2_sc = [tile([P, len(blocks) * P], U8, f"w2_sc{blocks[0]}") for blocks in W2_GROUPS]
         out_v = out.rearrange("(a p) s -> p a s", p=P)
 
         def scale(q):
@@ -176,11 +176,12 @@ def tile_picked_clnorm_relu_p_kernel(tc, x_words, x_scales, w1, mu, rs, w2, offs
         def second_product(s0, n, blocks, bank):
             acc = ps.tile([P, 512], F32, name=f"acc{s0}_{blocks[0]}", tag=bank)
             for i, b in enumerate(blocks):
-                cols = slice(b % 2 * P, (b % 2 + 1) * P)
+                c = b // 3
+                cols = slice((b - W2_GROUPS[c][0]) * P, (b - W2_GROUPS[c][0] + 1) * P)
                 nc.tensor.matmul_mx(
                     out=acc[:, i * n : (i + 1) * n],
-                    lhsT=w2_codes[b // 2][:, cols].bitcast(FP8X4),
-                    lhsT_scale=w2_sc[b // 2][:, cols],
+                    lhsT=w2_codes[c][:, cols].bitcast(FP8X4),
+                    lhsT_scale=w2_sc[c][:, cols],
                     rhs=z_codes[:, s0 : s0 + n].bitcast(FP8X4),
                     rhs_scale=z_sc[:, s0 : s0 + n],
                     start=True,
@@ -194,28 +195,29 @@ def tile_picked_clnorm_relu_p_kernel(tc, x_words, x_scales, w1, mu, rs, w2, offs
             copy_out(res[:].rearrange("p a s -> p (a s)"), acc[:, : len(blocks) * n])
             queue.dma_start(out_v[:, blocks[0] : blocks[-1] + 1, s0 : s0 + n], res[:])
 
-        w2_bf.append(tile([P, N // 2 * PACK], BF16, "w2_bf0", "w1_raw1"))
-        nc.scalar.activation(*interleaved(w2_bf[0][:], w2_raw[0][:]), ACT.Copy)
+        w2_bf.append(tile([P, 3 * P * PACK], BF16, "w2_bf0", "w1_raw1"))
+        for b in W2_GROUPS[0]:
+            nc.scalar.activation(*interleaved(w2_bf[0][:, b * P * PACK : (b + 1) * P * PACK], w2_raw[b][:]), ACT.Copy)
         z_bf = tile([P, 4, QUARTER * PACK], BF16, "z_bf")
         scale(0)
         scale(1)
-        w2_codes.append(tile([P, N // 2], U32, "w2_codes0", "scaled0"))
+        w2_codes.append(tile([P, 3 * P], U32, "w2_codes0", "scaled0"))
         quantize(w2_codes[0][:], w2_sc[0][:], w2_bf[0][:])
         scale(2)
         scale(3)
         for q in range(4):
             relu(q, z_bf[:, q, :])
         quantize_z(z_bf[:, :2, :].rearrange("p q c -> p (q c)"), 0, HALF)
-        w2_bf.append(tile([P, N // 2 * PACK], BF16, "w2_bf1", "scaled2"))
-        nc.vector.tensor_copy(*interleaved(w2_bf[1][:], w2_raw[1][:]))
+        w2_bf.append(tile([P, P * PACK], BF16, "w2_bf3", "scaled2"))
+        nc.vector.tensor_copy(*interleaved(w2_bf[1][:], w2_raw[3][:]))
         quantize_z(z_bf[:, 2, :], HALF, QUARTER)
-        w2_codes.append(tile([P, N // 2], U32, "w2_codes1"))
+        w2_codes.append(tile([P, P], U32, "w2_codes3"))
         quantize(w2_codes[1][:], w2_sc[1][:], w2_bf[1][:])
         quantize_z(z_bf[:, 3, :], HALF + QUARTER, QUARTER)
         store(second_product(0, HALF, (0,), "y0"), nc.scalar.copy, nc.sync)
         store(second_product(0, HALF, (1,), "y1"), nc.scalar.copy, nc.sync)
-        store(second_product(HALF, QUARTER, (0, 1), "y2"), nc.scalar.copy, nc.sync)
         store(second_product(0, HALF, (2,), "y3"), nc.scalar.copy, nc.sync)
-        store(second_product(HALF + QUARTER, QUARTER, (0, 1), "z0"), nc.scalar.copy, nc.sync)
-        store(second_product(0, S, (3,), "z1"), nc.vector.tensor_copy, nc.sync)
-        store(second_product(HALF, HALF, (2,), "z2"), nc.scalar.copy, nc.scalar)
+        store(second_product(0, HALF, (3,), "z0"), nc.vector.tensor_copy, nc.sync)
+        store(second_product(HALF, QUARTER, (0, 1, 2, 3), "y2"), nc.scalar.copy, nc.sync)
+        store(second_product(HALF + QUARTER, QUARTER, (0, 1), "z1"), nc.vector.tensor_copy, nc.sync)
+        store(second_product(HALF + QUARTER, QUARTER, (2, 3), "z2"), nc.scalar.copy, nc.scalar)

@@ -201,10 +201,10 @@ def tile_picked_clnorm_relu_p_kernel(tc, x_words, x_scales, w1, mu, rs, w2, offs
         z_bf = tile([P, 4, QUARTER * PACK], BF16, "z_bf")
         scale(0)
         scale(1)
-        w2_codes.append(tile([P, 3 * P], U32, "w2_codes0", "scaled0"))
-        quantize(w2_codes[0][:], w2_sc[0][:], w2_bf[0][:])
         scale(2)
         scale(3)
+        w2_codes.append(tile([P, 3 * P], U32, "w2_codes0", "scaled1"))
+        quantize(w2_codes[0][:], w2_sc[0][:], w2_bf[0][:])
         for q in range(4):
             relu(q, z_bf[:, q, :])
         quantize_z(z_bf[:, :2, :].rearrange("p q c -> p (q c)"), 0, HALF)

from contextlib import ExitStack

import concourse.mybir as mybir
from concourse.masks import make_identity

K, T, S, N, H, U = 1024, 2048, 512, 512, 512, 512
FLOPS = 2 * K * H * S + 2 * H * N * S

F32 = mybir.dt.float32
BF16 = mybir.dt.bfloat16
I32 = mybir.dt.int32
U32 = mybir.dt.uint32
U16 = mybir.dt.uint16
U8 = mybir.dt.uint8
FP8X4 = mybir.dt.float8_e4m3fn_x4
ALU = mybir.AluOpType
ACT = mybir.ActivationFunctionType

P = 128
PACK = 4
PASSES = K // (P * PACK)
HALF = S // 2
QUARTER = S // 4
W2_GROUPS = ((0, 1, 2), (3,))


def tile_picked_clnorm_relu_p_kernel(tc, x_words, x_scales, w1, mu, rs, w2, offs, cl, out):
    nc = tc.nc
    with ExitStack() as ctx:
        sb = ctx.enter_context(tc.tile_pool(name="sb", bufs=1))
        ps = ctx.enter_context(tc.psum_pool(name="ps", bufs=1))

        def tile(shape, dtype, name, tag=None):
            return sb.tile(shape, dtype, name=name, tag=tag or name, align_bytes=64)

        offs_t = sb.tile([P, S // 16], U16, name="offs_t")
        cl_t = sb.tile([P, S // 16], U16, name="cl_t")
        xs_all = tile([P, T], U8, "xs_all")
        xw_all = [tile([P, T], U32, f"xw_all{g}") for g in range(PASSES)]
        w1_raw = [tile([P, PACK, H], F32, f"w1_raw{g}") for g in range(PASSES)]
        w2_raw = [tile([P, PACK, P], F32, f"w2_raw{b}") for b in range(4)]
        mu_t = [tile([P, 2 * U], F32, f"mu{t}") for t in range(PACK)]
        rs_t = [tile([P, 2 * U], F32, f"rs{t}") for t in range(PACK)]
        ident = tile([P, P], F32, "ident")

        one = tile([P, 1], F32, "one")
        minus_one = tile([P, 1], F32, "minus_one")
        nc.vector.memset(one[:], 1.0)
        nc.scalar.activation(minus_one[:], one[:], ACT.Copy, scale=-1.0)
        nc.vector.memset(xs_all[:].bitcast(I32), 0)
        make_identity(nc, ident[:])

        mu_v = mu.rearrange("(p t) u -> p t u", t=PACK)
        rs_v = rs.rearrange("(p t) u -> p t u", t=PACK)
        w1_v = w1.rearrange("(g p j) c -> g p j c", g=PASSES, j=PACK)
        w2_v = w2.rearrange("(p j) c -> p j c", j=PACK)

        for q in range(4):
            (nc.scalar if q == 0 else nc.gpsimd).dma_start(
                xs_all[32 * q : 32 * q + 4 * PASSES, :].bitcast(I32),
                x_scales[:, 4 * q : 4 * q + 4, :].bitcast(I32),
            )
        nc.sync.dma_start(rs_t[0][:, :U], rs_v[:, 0, :])
        nc.sync.dma_start(cl_t[:], cl)
        for t in range(1, PACK):
            nc.sync.dma_start(rs_t[t][:, :U], rs_v[:, t, :])
            nc.sync.dma_start(mu_t[t - 1][:, :U], mu_v[:, t - 1, :])
        nc.sync.dma_start(mu_t[PACK - 1][:, :U], mu_v[:, PACK - 1, :])
        nc.sync.dma_start(offs_t[:], offs)
        nc.sync.dma_start(w1_raw[0][:], w1_v[0])
        nc.sync.dma_start(w1_raw[1][:], w1_v[1])
        for g in range(PASSES):
            nc.sync.dma_start(xw_all[g][:].bitcast(I32), x_words[g].rearrange("p c r -> p (c r)").bitcast(I32))
        for b in range(4):
            nc.sync.dma_start(w2_raw[b][:], w2_v[:, :, b * P : (b + 1) * P])

        def entries(lst, s0, n):
            return lst[:, s0 // 16 : (s0 + n) // 16]

        def look_up(table, t, name):
            picked = tile([P, S], F32, name)
            if t != 1:
                nc.scalar.activation(picked[:], table[:].indirect(cl_t[:]), ACT.Copy)
            else:
                nc.vector.tensor_copy(picked[:], table[:].indirect(cl_t[:]))
            return picked

        def turn(blocks, name, bank):
            turned = ps.tile([P, 4, P], F32, name=name, tag=bank)
            for i, block in enumerate(blocks):
                nc.tensor.transpose(turned[:, i, :], block, ident[:])
            return turned

        def add_turned(dst, src, start, stop):
            nc.tensor.matmul(dst, lhsT=src, rhs=ident[:], start=start, stop=stop, is_transpose=True)

        rs_g = [look_up(rs_t[t], t, f"rs_g{t}") for t in range(PACK)]
        rs_turned = [turn([rs_g[t][:, q * P : (q + 1) * P] for q in range(4)], f"rs_turned{t}", f"y{t}") for t in range(PACK)]
        mu_rs = [tile([P, S], F32, f"mu_rs{t}") for t in range(PACK)]
        for t in range(PACK):
            nc.vector.tensor_tensor(mu_rs[t][:], mu_t[t][:].indirect(cl_t[:]), rs_g[t][:], ALU.mult)
        rs_tok = tile([P, 4, PACK, P], F32, "rs_tok", "rs3")
        for t in range(PACK):
            nc.scalar.copy(rs_tok[:, :, t, :], rs_turned[t][:])
        mu_turned = [turn([mu_rs[t][:, q * P : (q + 1) * P] for q in range(4)], f"mu_turned{t}", f"z{t}") for t in range(PACK)]
        shift = [tile([P, 4, P], F32, f"shift{t}") for t in range(PACK)]
        for t in range(PACK):
            nc.scalar.activation(shift[t][:], mu_turned[t][:], ACT.Copy, scale=minus_one[:])
        z_pre = [ps.tile([P, PACK, P], F32, name=f"z_pre{q}", tag=f"z{q}") for q in range(4)]
        for t in range(PACK):
            for q in range(4):
                add_turned(z_pre[q][:, t, :], shift[t][:, q, :], t == 0, False)

        w1_codes = []
        w1_sc = [tile([P, H], U8, f"w1_sc{g}") for g in range(PASSES)]
        w1_bf = [tile([P, H * PACK], BF16, f"w1_bf{g}", ("mu3", "mu_rs3")[g]) for g in range(PASSES)]

        def quantize(codes, scales, src):
            nc.vector.quantize_mx(out=codes.bitcast(FP8X4), scales=scales, in_=src)

        def interleaved(dst, src):
            return dst.rearrange("p (c i t) -> p c t i", i=4, t=PACK), src.rearrange("p t (c i) -> p c t i", i=4)

        nc.vector.tensor_copy(*interleaved(w1_bf[0][:], w1_raw[0][:]))
        nc.scalar.activation(*interleaved(w1_bf[1][:], w1_raw[1][:]), ACT.Copy)
        xs = tile([P, S], U8, "xs", "w1_raw0")
        nc.vector.tensor_copy(xs[:], xs_all[:].indirect(offs_t[:]))
        w1_codes.append(tile([P, H], U32, "w1_codes0", "xs_all"))
        quantize(w1_codes[0][:], w1_sc[0][:], w1_bf[0][:])
        y = [ps.tile([P, H], F32, name=f"y{q}", tag=f"y{q}") for q in range(4)]

        def first_product(g, quarters, words):
            nc.vector.tensor_copy(words, xw_all[g][:].indirect(entries(offs_t, quarters[0] * P, len(quarters) * P)))
            for b, q in enumerate(quarters):
                nc.tensor.matmul_mx(
                    out=y[q][:],
                    lhsT=words[:, b * P : (b + 1) * P].bitcast(FP8X4),
                    lhsT_scale=xs[4 * g : P, q * P : (q + 1) * P],
                    rhs=w1_codes[g][:].bitcast(FP8X4),
                    rhs_scale=w1_sc[g][:],
                    start=(g == 0),
                    stop=(g == PASSES - 1),
                )

        xw0 = tile([P, S], U32, "xw0", "mu3")
        first_product(0, (0,), xw0[:, :P])
        first_product(0, (1,), xw0[:, P:HALF])
        first_product(0, (2, 3), xw0[:, HALF:])
        w1_codes.append(tile([P, H], U32, "w1_codes1"))
        quantize(w1_codes[1][:], w1_sc[1][:], w1_bf[1][:])
        first_product(1, (0,), tile([P, P], U32, "xw1_0")[:])
        first_product(1, (1, 2, 3), tile([P, 3 * P], U32, "xw1_1")[:])

        w2_bf = []
        w2_codes = []
        w2_sc = [tile([P, len(blocks) * P], U8, f"w2_sc{blocks[0]}") for blocks in W2_GROUPS]
        out_v = out.rearrange("(a p) s -> p a s", p=P)

        def scale(q):
            scaled = tile([P, PACK, P], F32, f"scaled{q}")
            nc.vector.tensor_tensor(scaled[:], y[q][:].rearrange("p (m t) -> p t m", t=PACK), rs_tok[:, q, :, :], ALU.mult)
            for t in range(PACK):
                add_turned(z_pre[q][:, t, :], scaled[:, t, :], False, t == PACK - 1)

        def relu(q, z_bf):
            nc.scalar.activation(
                out=z_bf.rearrange("p (s t) -> p s t", t=PACK), in_=z_pre[q][:].rearrange("p t s -> p s t"), func=ACT.Relu
            )

        z_codes = tile([P, S], U32, "z_codes")
        z_sc = tile([P, S], U8, "z_sc")

        def quantize_z(z_bf, s0, n):
            quantize(z_codes[:, s0 : s0 + n], z_sc[:, s0 : s0 + n], z_bf)

        def second_product(s0, n, blocks, bank):
            acc = ps.tile([P, 512], F32, name=f"acc{s0}_{blocks[0]}", tag=bank)
            for i, b in enumerate(blocks):
                c = b // 3
                cols = slice((b - W2_GROUPS[c][0]) * P, (b - W2_GROUPS[c][0] + 1) * P)
                nc.tensor.matmul_mx(
                    out=acc[:, i * n : (i + 1) * n],
                    lhsT=w2_codes[c][:, cols].bitcast(FP8X4),
                    lhsT_scale=w2_sc[c][:, cols],
                    rhs=z_codes[:, s0 : s0 + n].bitcast(FP8X4),
                    rhs_scale=z_sc[:, s0 : s0 + n],
                    start=True,
                    stop=True,
                )
            return acc, s0, n, blocks

        def store(product, copy_out, queue):
            acc, s0, n, blocks = product
            res = tile([P, len(blocks), n], F32, f"res{s0}_{blocks[0]}")
            copy_out(res[:].rearrange("p a s -> p (a s)"), acc[:, : len(blocks) * n])
            queue.dma_start(out_v[:, blocks[0] : blocks[-1] + 1, s0 : s0 + n], res[:])

        w2_bf.append(tile([P, 3 * P * PACK], BF16, "w2_bf0", "w1_raw1"))
        for b in W2_GROUPS[0]:
            nc.scalar.activation(*interleaved(w2_bf[0][:, b * P * PACK : (b + 1) * P * PACK], w2_raw[b][:]), ACT.Copy)
        z_bf = tile([P, 4, QUARTER * PACK], BF16, "z_bf")
        scale(0)
        scale(1)
        scale(2)
        scale(3)
        w2_codes.append(tile([P, 3 * P], U32, "w2_codes0", "scaled1"))
        quantize(w2_codes[0][:], w2_sc[0][:], w2_bf[0][:])
        for q in range(4):
            relu(q, z_bf[:, q, :])
        quantize_z(z_bf[:, :2, :].rearrange("p q c -> p (q c)"), 0, HALF)
        w2_bf.append(tile([P, P * PACK], BF16, "w2_bf3", "scaled2"))
        nc.vector.tensor_copy(*interleaved(w2_bf[1][:], w2_raw[3][:]))
        quantize_z(z_bf[:, 2, :], HALF, QUARTER)
        w2_codes.append(tile([P, P], U32, "w2_codes3"))
        quantize(w2_codes[1][:], w2_sc[1][:], w2_bf[1][:])
        quantize_z(z_bf[:, 3, :], HALF + QUARTER, QUARTER)
        store(second_product(0, HALF, (0,), "y0"), nc.scalar.copy, nc.sync)
        store(second_product(0, HALF, (1,), "y1"), nc.scalar.copy, nc.sync)
        store(second_product(0, HALF, (2,), "y3"), nc.scalar.copy, nc.sync)
        store(second_product(0, HALF, (3,), "z0"), nc.vector.tensor_copy, nc.sync)
        store(second_product(HALF, QUARTER, (0, 1, 2, 3), "y2"), nc.scalar.copy, nc.sync)
        store(second_product(HALF + QUARTER, QUARTER, (0, 1), "z1"), nc.vector.tensor_copy, nc.sync)
        store(second_product(HALF + QUARTER, QUARTER, (2, 3), "z2"), nc.scalar.copy, nc.scalar)
